import numpy as np
import ml_dtypes


def mxq(x, axis, fmt="e4m3"):
    dtype, down = {"e4m3": (ml_dtypes.float8_e4m3fn, 7), "e5m2": (ml_dtypes.float8_e5m2, 14)}[fmt]
    v = np.moveaxis(np.asarray(x, np.float32).astype(ml_dtypes.bfloat16).astype(np.float64), axis, -1)
    blocks = v.reshape(v.shape[:-1] + (-1, 32))
    amax = np.abs(blocks).max(-1, keepdims=True)
    byte = np.maximum(np.where(amax > 0, np.frexp(amax)[1] - 1 + 127, 0) - down, 1)
    scale = np.exp2(byte - 127.0)
    codes = (blocks / scale).astype(np.float32).astype(dtype).astype(np.float64)
    return np.moveaxis((codes * scale).reshape(v.shape), -1, axis)


WIDE = False


def mx_kscale(k):
    if not WIDE:
        return np.ones(k)
    levels = np.array([10, -10, 5, -5, 0])
    if k % 512:
        return np.exp2(np.random.permutation(np.resize(levels, k // 32))).repeat(32)
    a = np.empty((k // 512, 16))
    for p in range(k // 512):
        a[p, :8] = np.random.permutation(np.resize(levels, 8))
        for g in range(8):
            far = levels[np.abs(levels - a[p, g]) >= 10]
            a[p, g + 8] = far[np.random.randint(len(far))]
    return np.exp2(a.ravel()).repeat(32)


def f64(x):
    return np.asarray(x).astype(np.float64)


def striped(idx):
    return np.tile(idx.reshape(-1, 16).T, (8, 1)).astype(np.uint16)


def unstriped(offs):
    return offs[:16].T.reshape(-1).astype(np.int64)


def pack_weight(w):
    k, n = w.shape
    w = f64(np.asarray(w, np.float32).astype(ml_dtypes.bfloat16)).reshape(k // 32, 32, n)
    amax = np.abs(w).max(1)
    byte = np.clip(np.where(amax > 0, np.frexp(amax)[1] - 1 + 127 - 7, 1), 1, 254)
    scaled = (w * np.exp2(127.0 - byte)[:, None, :]).reshape(k, n).astype(np.float32)
    words = np.ascontiguousarray(scaled.reshape(k // 512, 128, 4, n).transpose(0, 1, 3, 2)).astype(ml_dtypes.float8_e4m3fn).view(np.uint8)
    return words, np.ascontiguousarray(byte.astype(np.uint8).reshape(k // 512, 16, n))


def unpack_weight(words, scales):
    g, p, n, _ = words.shape
    vals = np.ascontiguousarray(words).view(ml_dtypes.float8_e4m3fn).astype(np.float64) * np.repeat(np.exp2(scales.astype(np.float64) - 127.0), 8, axis=1)[..., None]
    return vals.transpose(0, 1, 3, 2).reshape(g * 512, n)


E2M1 = np.array([0.0, 0.5, 1.0, 1.5, 2.0, 3.0, 4.0, 6.0, -0.0, -0.5, -1.0, -1.5, -2.0, -3.0, -4.0, -6.0])


def pack_fp4(w):
    k, n = w.shape
    w = f64(np.asarray(w, np.float32).astype(ml_dtypes.bfloat16)).reshape(k // 32, 32, n)
    amax = np.abs(w).max(1)
    mant, ex = np.frexp(amax / 6.0)
    byte = np.clip(np.where(amax > 0, np.where(mant > 0.5, ex, ex - 1) + 127, 1), 1, 254)
    scaled = (w * np.exp2(127.0 - byte)[:, None, :]).reshape(k, n).astype(np.float32)
    c = np.ascontiguousarray(scaled.reshape(k // 512, 128, 4, n).transpose(0, 1, 3, 2)).astype(ml_dtypes.float4_e2m1fn).view(np.uint8) & 0xF
    words = (c[..., 0::2] | (c[..., 1::2] << 4)).reshape(k // 512, 128, 2 * n)
    return np.ascontiguousarray(words), np.ascontiguousarray(byte.astype(np.uint8).reshape(k // 512, 16, n))


def unpack_fp4(words, scales):
    g, _, n = scales.shape
    words = np.ascontiguousarray(words).reshape(g, 128, n, 2)
    nib = np.empty((g, 128, n, 4), np.uint8)
    nib[..., 0::2] = words & 0xF
    nib[..., 1::2] = words >> 4
    vals = E2M1[nib] * np.repeat(np.exp2(scales.astype(np.float64) - 127.0), 8, axis=1)[..., None]
    return vals.transpose(0, 1, 3, 2).reshape(g * 512, n)


def planes(y):
    n, m = y.shape
    v = y.astype(np.float32).astype(ml_dtypes.bfloat16).astype(np.float64).reshape(n // 32, 32, m)
    top = np.abs(v).max(1)
    byte = np.clip(np.where(top > 0, np.frexp(top)[1] - 1 + 127 - 7, 1), 1, 254)
    codes = (v * np.exp2(127.0 - byte)[:, None, :]).reshape(n, m).astype(np.float32).astype(ml_dtypes.float8_e4m3fn).view(np.uint8)
    words = codes.reshape(n // 512, 128, 4, m).transpose(0, 1, 3, 2)
    return np.ascontiguousarray(words), np.ascontiguousarray(byte.astype(np.uint8).reshape(n // 512, 16, m))


def relu(v):
    return np.maximum(v, 0.0)


K, T, S, D, V, H = 1024, 2048, 1024, 3, 512, 512
P = 2 ** 7


def setup_inputs():
    n = np.random.standard_normal
    s = mx_kscale(K)[:, None]
    u = mx_kscale(H)
    near = np.random.permutation(S)
    packed_xT = pack_weight(n((K, T)) * s)
    packed_w2 = pack_fp4(n((H, H)) / np.sqrt(H) / u[:, None])
    return {
        "x_words": packed_xT[0],
        "x_scales": packed_xT[1],
        "w1": (n((K, H)) / np.sqrt(K) / s * u).astype(np.float32),
        "w2_words": packed_w2[0],
        "w2_scales": packed_w2[1],
        "gate": (np.tile(np.random.uniform(0.2, 1.0, (D, 1, V)) / np.sqrt(D), (1, P, 1))).astype(np.float32),
        "turn": (np.random.uniform(0.5, 1.5, (H, 1)) * u[:, None]).astype(np.float32),
        "offs": striped(np.random.permutation(T)[:S]),
        "cen": striped(np.random.permutation(S)[:V]),
        "pos1": striped(near[:V]),
        "pos2": striped(near[V:]),
        "pos3": striped(np.random.permutation(S)[:V]),
    }


def reference(x_words, x_scales, w1, w2_words, w2_scales, gate, turn, offs, cen, pos1, pos2, pos3):
    xq = unpack_weight(x_words, x_scales)[:, unstriped(offs)]
    h = relu(mxq(f64(w1), 0, "e4m3").T @ xq)
    z = 0.9 * (h[:, unstriped(pos1)] * f64(gate)[0, :1] + h[:, unstriped(pos2)] * f64(gate)[1, :1] + h[:, unstriped(pos3)] * f64(gate)[2, :1]) + 0.1 * h[:, unstriped(cen)]
    y = unpack_fp4(w2_words, w2_scales).T @ mxq(z, 0, "e4m3")
    out_0 = 0.6 * z + 0.4 * (f64(turn) * y)
    return (out_0,) + planes(out_0)

@@ -1,0 +1,340 @@
+from contextlib import ExitStack
+
+import concourse.mybir as mybir
+from concourse.masks import make_identity
+
+K, T, S, D, V, H = 1024, 2048, 1024, 3, 512, 512
+FLOPS = 2 * K * H * S + 2 * H * H * V
+
+F32 = mybir.dt.float32
+BF16 = mybir.dt.bfloat16
+I32 = mybir.dt.int32
+U32 = mybir.dt.uint32
+U16 = mybir.dt.uint16
+U8 = mybir.dt.uint8
+FP8X4 = mybir.dt.float8_e4m3fn_x4
+FP4X4 = mybir.dt.float4_e2m1fn_x4
+MULT = mybir.AluOpType.mult
+ADD = mybir.AluOpType.add
+COPY = mybir.ActivationFunctionType.Copy
+RELU = mybir.ActivationFunctionType.Relu
+
+P = 128
+PACK = 4
+PASSES = K // (P * PACK)
+BANK = 512
+LIST = 16
+ROW_TILES = H // P
+CHUNKS = ((0, 384), (384, 128))
+SLOT = CHUNKS[0][1]
+CAST = P * PACK // 2
+RING = 2
+H_SCALE = 0.6 * 0.1
+GATE_SCALE = 0.9 / 0.1
+Z_SCALE = 1.0 / 0.6
+Y_SCALE = 0.4
+
+
+def pieces(width):
+    return [(o, min(256, width - o)) for o in range(0, width, 256)]
+
+
+def tile_picked_zgcnii_relu_po_kernel(
+    tc, x_words, x_scales, w1, w2_words, w2_scales, gate, turn, offs, cen, pos1, pos2, pos3, out_0, out_1, out_2
+):
+    nc = tc.nc
+    with ExitStack() as ctx:
+        lists = ctx.enter_context(tc.tile_pool(name="lists", bufs=1))
+        keep = ctx.enter_context(tc.tile_pool(name="keep", bufs=1))
+        psum_mx = ctx.enter_context(tc.psum_pool(name="psum_mx", bufs=6))
+        psum_tr = ctx.enter_context(tc.psum_pool(name="psum_tr", bufs=1))
+
+        def load_list(name, src):
+            held = lists.tile([P, src.shape[1]], U16, name=name)
+            nc.sync.dma_start(held[:], src)
+            return held
+
+        xs_raw = keep.tile([P, T], U8, name="xs_raw", align_bytes=64)
+        nc.gpsimd.memset(xs_raw[:].bitcast(I32), 0)
+        w2s_raw = keep.tile([P, H], U8, name="w2s_raw", align_bytes=64)
+        nc.gpsimd.memset(w2s_raw[:].bitcast(I32), 0)
+        ident = keep.tile([P, P], F32, name="ident")
+        make_identity(nc, ident[:])
+
+        offs_sb = load_list("offs_sb", offs)
+        gate_cols = keep.tile([P, D, PACK], F32, name="gate_cols")
+        nc.sync.dma_start(gate_cols[:], gate[:, 0, :].rearrange("d (p b) -> p d b", b=PACK))
+        for q in range(4):
+            nc.sync.dma_start(
+                xs_raw[32 * q : 32 * q + 4 * PASSES, :].bitcast(I32),
+                x_scales[:, 4 * q : 4 * q + 4, :].bitcast(I32),
+            )
+
+        w1_raw = {}
+
+        def load_w1(g, u):
+            raw = keep.tile([P, PACK, P], F32, name=f"w1_raw{g}_{u}", align_bytes=64)
+            rows = w1[g * P * PACK : (g + 1) * P * PACK, :].rearrange("(p j) c -> p j c", j=PACK)
+            nc.sync.dma_start(raw[:], rows[:, :, u * P : (u + 1) * P])
+            w1_raw[g, u] = raw
+
+        w2w_raw = keep.tile([P, 2 * H], U8, name="w2w_raw", align_bytes=64)
+        turn_sb = keep.tile([P, PACK], F32, name="turn_sb")
+
+        def load_w2():
+            nc.sync.dma_start(w2w_raw[:].bitcast(I32), w2_words[0].bitcast(I32))
+            for q in range(4):
+                nc.sync.dma_start(
+                    w2s_raw[32 * q : 32 * q + 4, :].bitcast(I32), w2_scales[0, 4 * q : 4 * q + 4, :].bitcast(I32)
+                )
+
+        xw_raw = []
+        for g in range(PASSES):
+            raw = keep.tile([P, T], I32, name=f"xw_raw{g}", align_bytes=64)
+            nc.sync.dma_start(raw[:], x_words[g].rearrange("p c r -> p (c r)").bitcast(I32))
+            xw_raw.append(raw)
+            if g == 0:
+                load_w1(0, 0)
+                load_w1(1, 0)
+        load_w1(0, 1)
+        load_w1(1, 1)
+        load_w2()
+        pos_sb = [load_list("pos1_sb", pos1)]
+        pos_sb.append(load_list("pos2_sb", pos2))
+        load_w1(0, 2)
+        load_w1(1, 2)
+        load_w1(0, 3)
+        cen_sb = load_list("cen_sb", cen)
+        pos_sb.append(load_list("pos3_sb", pos3))
+        load_w1(1, 3)
+        nc.sync.dma_start(turn_sb[:], turn.rearrange("(p t) o -> p (t o)", t=PACK))
+
+        ring = keep.tile([P, RING * (D + 1) * SLOT], F32, name="ring", align_bytes=64)
+
+        def ring_half(unit):
+            base = (unit % RING) * (D + 1) * SLOT
+            return ring[:, base : base + (D + 1) * SLOT]
+
+        turn_scaled = keep.tile([P, PACK], F32, name="turn_scaled")
+        nc.scalar.activation(turn_scaled[:], turn_sb[:], COPY, scale=Y_SCALE)
+
+        def interleave(planes, packed):
+            return (
+                packed.rearrange("p (c i) t -> p c t i", i=4),
+                planes.rearrange("p t (c i) -> p c t i", i=4),
+            )
+
+        w1_mx = {}
+
+        def quantise_w1(parts, staging):
+            cols = len(parts) * P
+            grouped = staging.bitcast(BF16)
+            name = "_".join(str(n) for n in parts[0])
+            codes = keep.tile([P, cols], U32, name=f"w1_codes{name}", align_bytes=64)
+            scales = keep.tile([P, cols], U8, name=f"w1_scales{name}", align_bytes=64)
+            for k, (g, u) in enumerate(parts):
+                packed = grouped[:, k * P * PACK : (k + 1) * P * PACK].rearrange("p (c j) -> p c j", j=PACK)
+                dst, src = interleave(w1_raw[g, u][:], packed)
+                nc.scalar.copy(dst, src)
+                w1_mx[g, u] = (codes[:, k * P : (k + 1) * P], scales[:, k * P : (k + 1) * P])
+            nc.vector.quantize_mx(out=codes[:].bitcast(FP8X4), scales=scales[:], in_=grouped)
+
+        xs = keep.tile([P, S], U8, name="xs", align_bytes=64)
+        nc.vector.tensor_copy(xs[:], xs_raw[:].indirect(offs_sb[:]))
+        xw = [keep.tile([P, S], U32, name=f"xw{g}", align_bytes=64) for g in range(PASSES)]
+        nc.vector.tensor_copy(xw[0][:], xw_raw[0][:].bitcast(U32).indirect(offs_sb[:]))
+        quantise_w1([(0, 0), (1, 0)], ring_half(1)[:, 0 : 2 * CAST])
+        for half in range(S // BANK):
+            nc.vector.tensor_copy(
+                xw[1][:, half * BANK : (half + 1) * BANK],
+                xw_raw[1][:].bitcast(U32).indirect(offs_sb[:, half * BANK // LIST : (half + 1) * BANK // LIST]),
+            )
+
+        gate_sb = [keep.tile([P, V], F32, name=f"gate{d}") for d in range(D)]
+
+        for d in range(D):
+            spread = psum_mx.tile([P, PACK, P], F32, name="acc")
+            for b in range(PACK):
+                nc.tensor.transpose(spread[:, b, :], gate_cols[:, d, b : b + 1].to_broadcast([P, P]), ident[:])
+            nc.scalar.activation(
+                gate_sb[d][:].rearrange("p (n b) -> p n b", b=PACK),
+                spread[:].rearrange("p b n -> p n b"),
+                COPY,
+                scale=GATE_SCALE,
+            )
+
+        h = []
+
+        def hidden_rows(u):
+            h_u = keep.tile([P, S], F32, name=f"h{u}")
+            for half in range(S // BANK):
+                cols = slice(half * BANK, (half + 1) * BANK)
+                acc = psum_mx.tile([P, BANK], F32, name="acc")
+                for g in range(PASSES):
+                    codes, scales = w1_mx[g, u]
+                    nc.tensor.matmul_mx(
+                        out=acc[:],
+                        lhsT=codes.bitcast(FP8X4),
+                        lhsT_scale=scales,
+                        rhs=xw[g][:, cols].bitcast(FP8X4),
+                        rhs_scale=xs[4 * g : P, cols],
+                        start=(g == 0),
+                        stop=(g == PASSES - 1),
+                    )
+                nc.scalar.activation(h_u[:, cols], acc[:], RELU, scale=H_SCALE)
+            h.append(h_u)
+
+        quantise_w1([(0, 1), (1, 1)], ring_half(0)[:, SLOT - 64 : SLOT - 64 + 2 * CAST])
+        hidden_rows(0)
+        hidden_rows(1)
+
+        w2w = keep.tile([P, PACK, P, 2], U8, name="w2w", align_bytes=64)
+        nc.vector.tensor_copy(w2w[:], w2w_raw[:].rearrange("p (m t b) -> p t m b", t=PACK, b=2))
+        w2s = keep.tile([P, PACK, P], U8, name="w2s", align_bytes=64)
+        nc.vector.tensor_copy(w2s[:], w2s_raw[:].rearrange("p (m t) -> p t m", t=PACK))
+
+        z_stage = keep.tile([P, SLOT * PACK // 2], F32, name="z_stage", align_bytes=64)
+        out_codes = keep.tile([P, V], U32, name="out_codes", align_bytes=64)
+        out_scales = keep.tile([P, V], U8, name="out_scales", align_bytes=64)
+        out_rows = out_0.rearrange("(p t) v -> p t v", t=PACK)
+        out_words = out_1[0].rearrange("p c r -> p (c r)").bitcast(I32)
+
+        def mix(n):
+            c0, width = CHUNKS[n]
+            blocks = width // P
+            lcols = slice(c0 // LIST, (c0 + width) // LIST)
+            cols = slice(c0, c0 + width)
+            z_flat = keep.tile([P, PACK * width], F32, name=f"z_turned{n}")
+            z_turned = z_flat[:].rearrange("v (b t p) -> v b t p", t=PACK, p=P)
+            for u in range(ROW_TILES):
+                if n == 0 and u == 1:
+                    quantise_w1([(0, 2), (1, 2), (0, 3), (1, 3)], ring_half(1)[:, 0 : 4 * CAST])
+                    hidden_rows(2)
+                    hidden_rows(3)
+                if n == 0:
+                    slot = [ring_half(u)[:, k * SLOT : (k + 1) * SLOT] for k in range(D + 1)]
+                elif u + 1 < ROW_TILES:
+                    slot = [ring_half(0)[:, (u * (D + 1) + k) * width : (u * (D + 1) + k + 1) * width] for k in range(D + 1)]
+                else:
+                    slot = [ring_half(1)[:, k * width : (k + 1) * width] if k < 2 else z_stage[:, k * width : (k + 1) * width] for k in range(D + 1)]
+                if n == 0:
+                    turned = psum_tr.tile([P, width], F32, name=f"turned{u % 2}")[:]
+                elif u == 0:
+                    early = psum_tr.tile([P, (ROW_TILES - 1) * width], F32, name="turned1")
+                if n == 1:
+                    if u + 1 < ROW_TILES:
+                        turned = early[:, u * width : (u + 1) * width]
+                    else:
+                        turned = psum_tr.tile([P, width], F32, name="turned0")[:]
+
+                def add_turned(term, first, final):
+                    for b in range(blocks):
+                        nc.tensor.matmul(
+                            turned[:, b * P : (b + 1) * P],
+                            term[:, b * P : (b + 1) * P],
+                            ident[:],
+                            start=(first and b == 0),
+                            stop=(final and b == blocks - 1),
+                            is_transpose=True,
+                        )
+
+                window = h[u][:]
+                nc.vector.tensor_tensor(slot[0], window.indirect(pos_sb[0][:, lcols]), gate_sb[0][:, cols], MULT)
+                nc.vector.tensor_tensor(slot[1], window.indirect(pos_sb[1][:, lcols]), gate_sb[1][:, cols], MULT)
+                add_turned(slot[1], True, False)
+                nc.vector.tensor_tensor(slot[3], window.indirect(cen_sb[:, lcols]), slot[0], ADD)
+                add_turned(slot[3], False, False)
+                nc.vector.tensor_tensor(slot[2], window.indirect(pos_sb[2][:, lcols]), gate_sb[2][:, cols], MULT)
+                add_turned(slot[2], False, True)
+                if n == 0 or u + 1 == ROW_TILES:
+                    nc.scalar.copy(
+                        z_turned[:, :, :, u * 32 : (u + 1) * 32],
+                        turned.rearrange("v (b q t) -> v b t q", t=PACK, q=32),
+                    )
+                elif u + 2 == ROW_TILES:
+                    nc.scalar.copy(
+                        z_turned[:, 0, :, 0 : (u + 1) * 32], early[:].rearrange("v (q t) -> v t q", t=PACK)
+                    )
+            return z_flat
+
+        def quantise_z(n, z_flat):
+            c0, width = CHUNKS[n]
+            z_turned = z_flat[:].rearrange("v (b t p) -> v b t p", t=PACK, p=P)
+            zs = z_flat[:].rearrange("p (t v) -> p t v", t=PACK)
+            if n == 0:
+                z_bf = z_stage[:].bitcast(BF16).rearrange("p (c t) -> p c t", t=PACK)
+            else:
+                z_bf = keep.tile([P, width, PACK], BF16, name=f"z_bf{n}", align_bytes=64)[:]
+            z_codes = keep.tile([P, width], U32, name=f"z_codes{n}", align_bytes=64)
+            z_scales = keep.tile([P, width], U8, name=f"z_scales{n}", align_bytes=64)
+            backs = []
+            for b in range(width // P):
+                back = psum_mx.tile([P, PACK, P], F32, name="acc")
+                for t in range(PACK):
+                    nc.tensor.transpose(back[:, t, :], z_turned[:, b, t, :], ident[:])
+                nc.scalar.activation(
+                    z_bf[:, b * P : (b + 1) * P, :], back[:].rearrange("p t v -> p v t"), COPY, scale=Z_SCALE
+                )
+                backs.append(back)
+            for o, w in pieces(width):
+                nc.vector.quantize_mx(
+                    out=z_codes[:, o : o + w].bitcast(FP8X4),
+                    scales=z_scales[:, o : o + w],
+                    in_=z_bf[:, o : o + w, :].rearrange("p c t -> p (c t)"),
+                )
+            for b, back in enumerate(backs):
+                nc.scalar.copy(zs[:, :, b * P : (b + 1) * P], back[:])
+            return zs, z_codes, z_scales
+
+        def second_product(n, zs, z_codes, z_scales):
+            c0, width = CHUNKS[n]
+            res = keep.tile([P, PACK, width], F32, name=f"res{n}")
+            for t in range(PACK):
+                y = psum_mx.tile([P, BANK], F32, name="acc")
+                for o, w in pieces(width):
+                    nc.tensor.matmul_mx(
+                        out=y[:, o : o + w],
+                        lhsT=w2w[:, t, :, :].rearrange("p m b -> p (m b)").bitcast(FP4X4),
+                        lhsT_scale=w2s[:, t, :],
+                        rhs=z_codes[:, o : o + w].bitcast(FP8X4),
+                        rhs_scale=z_scales[:, o : o + w],
+                        start=True,
+                        stop=True,
+                    )
+                nc.vector.scalar_tensor_tensor(
+                    res[:, t, :], y[:, 0:width], turn_scaled[:, t : t + 1], zs[:, t, :], MULT, ADD
+                )
+            nc.sync.dma_start(out_rows[:, :, c0 : c0 + width], res[:])
+            return res
+
+        def result_planes(n, res, on_vector):
+            c0, width = CHUNKS[n]
+            res_bf = keep.tile([P, width, PACK], BF16, name=f"res_bf{n}", align_bytes=64)
+            for b in range(width // P):
+                dst, src = interleave(res[:, :, b * P : (b + 1) * P], res_bf[:, b * P : (b + 1) * P, :])
+                if on_vector:
+                    nc.vector.tensor_copy(dst, src)
+                else:
+                    nc.scalar.copy(dst, src)
+            for o, w in pieces(width):
+                nc.vector.quantize_mx(
+                    out=out_codes[:, c0 + o : c0 + o + w].bitcast(FP8X4),
+                    scales=out_scales[:, c0 + o : c0 + o + w],
+                    in_=res_bf[:, o : o + w, :].rearrange("p c t -> p (c t)"),
+                )
+            nc.sync.dma_start(out_words[:, c0 : c0 + width], out_codes[:, c0 : c0 + width].bitcast(I32))
+
+        turned0 = mix(0)
+        z0 = quantise_z(0, turned0)
+        turned1 = mix(1)
+        res0 = second_product(0, *z0)
+        z1 = quantise_z(1, turned1)
+        result_planes(0, res0, False)
+        res1 = second_product(1, *z1)
+        result_planes(1, res1, True)
+
+        for q in range(4):
+            queue = nc.sync if q % 2 == 0 else nc.scalar
+            queue.dma_start(
+                out_2[0, 4 * q : 4 * q + 4, :].bitcast(I32), out_scales[32 * q : 32 * q + 4, :].bitcast(I32)
+            )

@@ -28,7 +28,7 @@ ROW_TILES = H // P
 CHUNKS = ((0, 384), (384, 128))
 SLOT = CHUNKS[0][1]
 CAST = P * PACK // 2
-RING = 2
+RING = 4
 H_SCALE = 0.6 * 0.1
 GATE_SCALE = 0.9 / 0.1
 Z_SCALE = 1.0 / 0.6
@@ -62,6 +62,8 @@ def tile_picked_zgcnii_relu_po_kernel(
         make_identity(nc, ident[:])
 
         offs_sb = load_list("offs_sb", offs)
+        w2w_raw = keep.tile([P, 2 * H], U8, name="w2w_raw", align_bytes=64)
+        nc.sync.dma_start(w2w_raw[:].bitcast(I32), w2_words[0].bitcast(I32))
         gate_cols = keep.tile([P, D, PACK], F32, name="gate_cols")
         nc.sync.dma_start(gate_cols[:], gate[:, 0, :].rearrange("d (p b) -> p d b", b=PACK))
         for q in range(4):
@@ -72,17 +74,15 @@ def tile_picked_zgcnii_relu_po_kernel(
 
         w1_raw = {}
 
-        def load_w1(g, u):
-            raw = keep.tile([P, PACK, P], F32, name=f"w1_raw{g}_{u}", align_bytes=64)
+        def load_w1(g, u, tiles=1):
+            raw = keep.tile([P, PACK, tiles * P], F32, name=f"w1_raw{g}_{u}", align_bytes=64)
             rows = w1[g * P * PACK : (g + 1) * P * PACK, :].rearrange("(p j) c -> p j c", j=PACK)
-            nc.sync.dma_start(raw[:], rows[:, :, u * P : (u + 1) * P])
+            nc.sync.dma_start(raw[:], rows[:, :, u * P : (u + tiles) * P])
             w1_raw[g, u] = raw
 
-        w2w_raw = keep.tile([P, 2 * H], U8, name="w2w_raw", align_bytes=64)
         turn_sb = keep.tile([P, PACK], F32, name="turn_sb")
 
         def load_w2():
-            nc.sync.dma_start(w2w_raw[:].bitcast(I32), w2_words[0].bitcast(I32))
             for q in range(4):
                 nc.sync.dma_start(
                     w2s_raw[32 * q : 32 * q + 4, :].bitcast(I32), w2_scales[0, 4 * q : 4 * q + 4, :].bitcast(I32)
@@ -98,22 +98,20 @@ def tile_picked_zgcnii_relu_po_kernel(
                 load_w1(1, 0)
         load_w1(0, 1)
         load_w1(1, 1)
+        load_w1(0, 2, 2)
         load_w2()
         pos_sb = [load_list("pos1_sb", pos1)]
         pos_sb.append(load_list("pos2_sb", pos2))
-        load_w1(0, 2)
-        load_w1(1, 2)
-        load_w1(0, 3)
         cen_sb = load_list("cen_sb", cen)
+        load_w1(1, 2, 2)
         pos_sb.append(load_list("pos3_sb", pos3))
-        load_w1(1, 3)
         nc.sync.dma_start(turn_sb[:], turn.rearrange("(p t) o -> p (t o)", t=PACK))
 
-        ring = keep.tile([P, RING * (D + 1) * SLOT], F32, name="ring", align_bytes=64)
+        ring = keep.tile([P, (1 + RING * D) * SLOT], F32, name="ring", align_bytes=64)
 
         def ring_half(unit):
-            base = (unit % RING) * (D + 1) * SLOT
-            return ring[:, base : base + (D + 1) * SLOT]
+            base = (1 + (unit % RING) * D) * SLOT
+            return ring[:, base : base + D * SLOT]
 
         turn_scaled = keep.tile([P, PACK], F32, name="turn_scaled")
         nc.scalar.activation(turn_scaled[:], turn_sb[:], COPY, scale=Y_SCALE)
@@ -126,24 +124,28 @@ def tile_picked_zgcnii_relu_po_kernel(
 
         w1_mx = {}
 
-        def quantise_w1(parts, staging):
-            cols = len(parts) * P
+        def quantise_w1(u0, tiles, staging):
+            cols = tiles * P
             grouped = staging.bitcast(BF16)
-            name = "_".join(str(n) for n in parts[0])
-            codes = keep.tile([P, cols], U32, name=f"w1_codes{name}", align_bytes=64)
-            scales = keep.tile([P, cols], U8, name=f"w1_scales{name}", align_bytes=64)
-            for k, (g, u) in enumerate(parts):
-                packed = grouped[:, k * P * PACK : (k + 1) * P * PACK].rearrange("p (c j) -> p c j", j=PACK)
-                dst, src = interleave(w1_raw[g, u][:], packed)
-                nc.scalar.copy(dst, src)
-                w1_mx[g, u] = (codes[:, k * P : (k + 1) * P], scales[:, k * P : (k + 1) * P])
+            codes = keep.tile([P, PASSES * cols], U32, name=f"w1_codes{u0}", align_bytes=64)
+            scales = keep.tile([P, PASSES * cols], U8, name=f"w1_scales{u0}", align_bytes=64)
+            for g in range(PASSES):
+                packed = grouped[:, g * cols * PACK : (g + 1) * cols * PACK].rearrange("p (c j) -> p c j", j=PACK)
+                dst, src = interleave(w1_raw[g, u0][:], packed)
+                if (g, u0) == (1, 1):
+                    nc.vector.tensor_copy(dst, src)
+                else:
+                    nc.scalar.copy(dst, src)
+                for k in range(tiles):
+                    place = slice(g * cols + k * P, g * cols + (k + 1) * P)
+                    w1_mx[g, u0 + k] = (codes[:, place], scales[:, place])
             nc.vector.quantize_mx(out=codes[:].bitcast(FP8X4), scales=scales[:], in_=grouped)
 
         xs = keep.tile([P, S], U8, name="xs", align_bytes=64)
         nc.vector.tensor_copy(xs[:], xs_raw[:].indirect(offs_sb[:]))
         xw = [keep.tile([P, S], U32, name=f"xw{g}", align_bytes=64) for g in range(PASSES)]
         nc.vector.tensor_copy(xw[0][:], xw_raw[0][:].bitcast(U32).indirect(offs_sb[:]))
-        quantise_w1([(0, 0), (1, 0)], ring_half(1)[:, 0 : 2 * CAST])
+        quantise_w1(0, 1, ring[:, 7 * SLOT - 2 * CAST : 7 * SLOT])
         for half in range(S // BANK):
             nc.vector.tensor_copy(
                 xw[1][:, half * BANK : (half + 1) * BANK],
@@ -184,7 +186,7 @@ def tile_picked_zgcnii_relu_po_kernel(
                 nc.scalar.activation(h_u[:, cols], acc[:], RELU, scale=H_SCALE)
             h.append(h_u)
 
-        quantise_w1([(0, 1), (1, 1)], ring_half(0)[:, SLOT - 64 : SLOT - 64 + 2 * CAST])
+        quantise_w1(1, 1, ring[:, SLOT - CAST : SLOT + CAST])
         hidden_rows(0)
         hidden_rows(1)
 
@@ -194,6 +196,8 @@ def tile_picked_zgcnii_relu_po_kernel(
         nc.vector.tensor_copy(w2s[:], w2s_raw[:].rearrange("p (m t) -> p t m", t=PACK))
 
         z_stage = keep.tile([P, SLOT * PACK // 2], F32, name="z_stage", align_bytes=64)
+        res_flat = keep.tile([P, V * PACK], BF16, name="res_bf", align_bytes=64)
+        res_bf = res_flat[:].rearrange("p (c t) -> p c t", t=PACK)
         out_codes = keep.tile([P, V], U32, name="out_codes", align_bytes=64)
         out_scales = keep.tile([P, V], U8, name="out_scales", align_bytes=64)
         out_rows = out_0.rearrange("(p t) v -> p t v", t=PACK)
@@ -207,16 +211,13 @@ def tile_picked_zgcnii_relu_po_kernel(
             z_flat = keep.tile([P, PACK * width], F32, name=f"z_turned{n}")
             z_turned = z_flat[:].rearrange("v (b t p) -> v b t p", t=PACK, p=P)
             for u in range(ROW_TILES):
-                if n == 0 and u == 1:
-                    quantise_w1([(0, 2), (1, 2), (0, 3), (1, 3)], ring_half(1)[:, 0 : 4 * CAST])
-                    hidden_rows(2)
-                    hidden_rows(3)
                 if n == 0:
-                    slot = [ring_half(u)[:, k * SLOT : (k + 1) * SLOT] for k in range(D + 1)]
+                    slot = [ring[:, 0:SLOT]] + [ring_half(u)[:, k * SLOT : (k + 1) * SLOT] for k in ((0, 2, 1), (0, 1, 2))[u % 2]]
                 elif u + 1 < ROW_TILES:
-                    slot = [ring_half(0)[:, (u * (D + 1) + k) * width : (u * (D + 1) + k + 1) * width] for k in range(D + 1)]
+                    places = [ring[:, 0:SLOT]] + [ring_half(2)[:, k * SLOT : (k + 1) * SLOT] for k in range(D)]
+                    slot = [places[k][:, u * width : (u + 1) * width] for k in range(D + 1)]
                 else:
-                    slot = [ring_half(1)[:, k * width : (k + 1) * width] if k < 2 else z_stage[:, k * width : (k + 1) * width] for k in range(D + 1)]
+                    slot = [z_stage[:, (k + 2) * width : (k + 3) * width] for k in range(D + 1)]
                 if n == 0:
                     turned = psum_tr.tile([P, width], F32, name=f"turned{u % 2}")[:]
                 elif u == 0:
@@ -241,9 +242,13 @@ def tile_picked_zgcnii_relu_po_kernel(
                 window = h[u][:]
                 nc.vector.tensor_tensor(slot[0], window.indirect(pos_sb[0][:, lcols]), gate_sb[0][:, cols], MULT)
                 nc.vector.tensor_tensor(slot[1], window.indirect(pos_sb[1][:, lcols]), gate_sb[1][:, cols], MULT)
-                add_turned(slot[1], True, False)
                 nc.vector.tensor_tensor(slot[3], window.indirect(cen_sb[:, lcols]), slot[0], ADD)
-                add_turned(slot[3], False, False)
+                add_turned(slot[3], True, False)
+                add_turned(slot[1], False, False)
+                if n == 0 and u == 0:
+                    quantise_w1(2, 2, ring[:, 4 * SLOT - P : 4 * SLOT - P + 4 * CAST])
+                    hidden_rows(2)
+                    hidden_rows(3)
                 nc.vector.tensor_tensor(slot[2], window.indirect(pos_sb[2][:, lcols]), gate_sb[2][:, cols], MULT)
                 add_turned(slot[2], False, True)
                 if n == 0 or u + 1 == ROW_TILES:
@@ -264,7 +269,7 @@ def tile_picked_zgcnii_relu_po_kernel(
             if n == 0:
                 z_bf = z_stage[:].bitcast(BF16).rearrange("p (c t) -> p c t", t=PACK)
             else:
-                z_bf = keep.tile([P, width, PACK], BF16, name=f"z_bf{n}", align_bytes=64)[:]
+                z_bf = res_bf[:, P // 2 : P // 2 + width, :]
             z_codes = keep.tile([P, width], U32, name=f"z_codes{n}", align_bytes=64)
             z_scales = keep.tile([P, width], U8, name=f"z_scales{n}", align_bytes=64)
             backs = []
@@ -286,9 +291,9 @@ def tile_picked_zgcnii_relu_po_kernel(
                 nc.scalar.copy(zs[:, :, b * P : (b + 1) * P], back[:])
             return zs, z_codes, z_scales
 
-        def second_product(n, zs, z_codes, z_scales):
-            c0, width = CHUNKS[n]
-            res = keep.tile([P, PACK, width], F32, name=f"res{n}")
+        def second_product(n, z_codes, z_scales):
+            width = CHUNKS[n][1]
+            banks = []
             for t in range(PACK):
                 y = psum_mx.tile([P, BANK], F32, name="acc")
                 for o, w in pieces(width):
@@ -301,37 +306,46 @@ def tile_picked_zgcnii_relu_po_kernel(
                         start=True,
                         stop=True,
                     )
+                banks.append(y)
+            return banks
+
+        def combine(n, zs, banks):
+            c0, width = CHUNKS[n]
+            res = keep.tile([P, PACK, width], F32, name=f"res{n}")
+            for t, y in enumerate(banks):
                 nc.vector.scalar_tensor_tensor(
                     res[:, t, :], y[:, 0:width], turn_scaled[:, t : t + 1], zs[:, t, :], MULT, ADD
                 )
             nc.sync.dma_start(out_rows[:, :, c0 : c0 + width], res[:])
             return res
 
-        def result_planes(n, res, on_vector):
+        def round_result(n, res, on_vector):
             c0, width = CHUNKS[n]
-            res_bf = keep.tile([P, width, PACK], BF16, name=f"res_bf{n}", align_bytes=64)
             for b in range(width // P):
-                dst, src = interleave(res[:, :, b * P : (b + 1) * P], res_bf[:, b * P : (b + 1) * P, :])
-                if on_vector:
+                dst, src = interleave(res[:, :, b * P : (b + 1) * P], res_bf[:, c0 + b * P : c0 + (b + 1) * P, :])
+                if b in on_vector:
                     nc.vector.tensor_copy(dst, src)
                 else:
                     nc.scalar.copy(dst, src)
-            for o, w in pieces(width):
-                nc.vector.quantize_mx(
-                    out=out_codes[:, c0 + o : c0 + o + w].bitcast(FP8X4),
-                    scales=out_scales[:, c0 + o : c0 + o + w],
-                    in_=res_bf[:, o : o + w, :].rearrange("p c t -> p (c t)"),
-                )
-            nc.sync.dma_start(out_words[:, c0 : c0 + width], out_codes[:, c0 : c0 + width].bitcast(I32))
 
-        turned0 = mix(0)
-        z0 = quantise_z(0, turned0)
+        def result_planes(cols):
+            nc.vector.quantize_mx(
+                out=out_codes[:, cols].bitcast(FP8X4),
+                scales=out_scales[:, cols],
+                in_=res_bf[:, cols, :].rearrange("p c t -> p (c t)"),
+            )
+            nc.sync.dma_start(out_words[:, cols], out_codes[:, cols].bitcast(I32))
+
+        zs0, z_codes0, z_scales0 = quantise_z(0, mix(0))
+        banks0 = second_product(0, z_codes0, z_scales0)
         turned1 = mix(1)
-        res0 = second_product(0, *z0)
-        z1 = quantise_z(1, turned1)
-        result_planes(0, res0, False)
-        res1 = second_product(1, *z1)
-        result_planes(1, res1, True)
+        res0 = combine(0, zs0, banks0)
+        zs1, z_codes1, z_scales1 = quantise_z(1, turned1)
+        round_result(0, res0, (0,))
+        res1 = combine(1, zs1, second_product(1, z_codes1, z_scales1))
+        result_planes(slice(0, V // 2))
+        round_result(1, res1, (0,))
+        result_planes(slice(V // 2, V))
 
         for q in range(4):
             queue = nc.sync if q % 2 == 0 else nc.scalar

@@ -28,6 +28,8 @@ ROW_TILES = H // P
 CHUNKS = ((0, 384), (384, 128))
 SLOT = CHUNKS[0][1]
 CAST = P * PACK // 2
+FIRST_CUTS = ((0, 512), (512, 768), (768, 1024))
+BANK_CUTS = ((0, 512), (512, 1024))
 RING = 4
 H_SCALE = 0.6 * 0.1
 GATE_SCALE = 0.9 / 0.1
@@ -60,6 +62,10 @@ def tile_picked_zgcnii_relu_po_kernel(
         nc.gpsimd.memset(w2s_raw[:].bitcast(I32), 0)
         ident = keep.tile([P, P], F32, name="ident")
         make_identity(nc, ident[:])
+        for q in range(4):
+            nc.gpsimd.dma_start(
+                w2s_raw[32 * q : 32 * q + 4, :].bitcast(I32), w2_scales[0, 4 * q : 4 * q + 4, :].bitcast(I32)
+            )
 
         offs_sb = load_list("offs_sb", offs)
         w2w_raw = keep.tile([P, 2 * H], U8, name="w2w_raw", align_bytes=64)
@@ -82,12 +88,6 @@ def tile_picked_zgcnii_relu_po_kernel(
 
         turn_sb = keep.tile([P, PACK], F32, name="turn_sb")
 
-        def load_w2():
-            for q in range(4):
-                nc.sync.dma_start(
-                    w2s_raw[32 * q : 32 * q + 4, :].bitcast(I32), w2_scales[0, 4 * q : 4 * q + 4, :].bitcast(I32)
-                )
-
         xw_raw = []
         for g in range(PASSES):
             raw = keep.tile([P, T], I32, name=f"xw_raw{g}", align_bytes=64)
@@ -99,7 +99,6 @@ def tile_picked_zgcnii_relu_po_kernel(
         load_w1(0, 1)
         load_w1(1, 1)
         load_w1(0, 2, 2)
-        load_w2()
         pos_sb = [load_list("pos1_sb", pos1)]
         pos_sb.append(load_list("pos2_sb", pos2))
         cen_sb = load_list("cen_sb", cen)
@@ -132,7 +131,7 @@ def tile_picked_zgcnii_relu_po_kernel(
             for g in range(PASSES):
                 packed = grouped[:, g * cols * PACK : (g + 1) * cols * PACK].rearrange("p (c j) -> p c j", j=PACK)
                 dst, src = interleave(w1_raw[g, u0][:], packed)
-                if (g, u0) == (1, 1):
+                if u0 == 1:
                     nc.vector.tensor_copy(dst, src)
                 else:
                     nc.scalar.copy(dst, src)
@@ -146,10 +145,9 @@ def tile_picked_zgcnii_relu_po_kernel(
         xw = [keep.tile([P, S], U32, name=f"xw{g}", align_bytes=64) for g in range(PASSES)]
         nc.vector.tensor_copy(xw[0][:], xw_raw[0][:].bitcast(U32).indirect(offs_sb[:]))
         quantise_w1(0, 1, ring[:, 7 * SLOT - 2 * CAST : 7 * SLOT])
-        for half in range(S // BANK):
+        for lo, hi in FIRST_CUTS:
             nc.vector.tensor_copy(
-                xw[1][:, half * BANK : (half + 1) * BANK],
-                xw_raw[1][:].bitcast(U32).indirect(offs_sb[:, half * BANK // LIST : (half + 1) * BANK // LIST]),
+                xw[1][:, lo:hi], xw_raw[1][:].bitcast(U32).indirect(offs_sb[:, lo // LIST : hi // LIST])
             )
 
         gate_sb = [keep.tile([P, V], F32, name=f"gate{d}") for d in range(D)]
@@ -169,9 +167,9 @@ def tile_picked_zgcnii_relu_po_kernel(
 
         def hidden_rows(u):
             h_u = keep.tile([P, S], F32, name=f"h{u}")
-            for half in range(S // BANK):
-                cols = slice(half * BANK, (half + 1) * BANK)
-                acc = psum_mx.tile([P, BANK], F32, name="acc")
+            for lo, hi in FIRST_CUTS if u == 0 else BANK_CUTS:
+                cols = slice(lo, hi)
+                acc = psum_mx.tile([P, hi - lo], F32, name="acc")
                 for g in range(PASSES):
                     codes, scales = w1_mx[g, u]
                     nc.tensor.matmul_mx(
@@ -193,7 +191,7 @@ def tile_picked_zgcnii_relu_po_kernel(
         w2w = keep.tile([P, PACK, P, 2], U8, name="w2w", align_bytes=64)
         nc.vector.tensor_copy(w2w[:], w2w_raw[:].rearrange("p (m t b) -> p t m b", t=PACK, b=2))
         w2s = keep.tile([P, PACK, P], U8, name="w2s", align_bytes=64)
-        nc.vector.tensor_copy(w2s[:], w2s_raw[:].rearrange("p (m t) -> p t m", t=PACK))
+        nc.gpsimd.tensor_copy(w2s[:], w2s_raw[:].rearrange("p (m t) -> p t m", t=PACK))
 
         z_stage = keep.tile([P, SLOT * PACK // 2], F32, name="z_stage", align_bytes=64)
         res_flat = keep.tile([P, V * PACK], BF16, name="res_bf", align_bytes=64)
@@ -319,14 +317,10 @@ def tile_picked_zgcnii_relu_po_kernel(
             nc.sync.dma_start(out_rows[:, :, c0 : c0 + width], res[:])
             return res
 
-        def round_result(n, res, on_vector):
-            c0, width = CHUNKS[n]
-            for b in range(width // P):
-                dst, src = interleave(res[:, :, b * P : (b + 1) * P], res_bf[:, c0 + b * P : c0 + (b + 1) * P, :])
-                if b in on_vector:
-                    nc.vector.tensor_copy(dst, src)
-                else:
-                    nc.scalar.copy(dst, src)
+        def round_result(copy, n, res, lo, hi):
+            c0 = CHUNKS[n][0]
+            dst, src = interleave(res[:, :, lo:hi], res_bf[:, c0 + lo : c0 + hi, :])
+            copy(dst, src)
 
         def result_planes(cols):
             nc.vector.quantize_mx(
@@ -341,10 +335,11 @@ def tile_picked_zgcnii_relu_po_kernel(
         turned1 = mix(1)
         res0 = combine(0, zs0, banks0)
         zs1, z_codes1, z_scales1 = quantise_z(1, turned1)
-        round_result(0, res0, (0,))
+        round_result(nc.vector.tensor_copy, 0, res0, 0, P)
+        round_result(nc.scalar.copy, 0, res0, P, SLOT)
         res1 = combine(1, zs1, second_product(1, z_codes1, z_scales1))
         result_planes(slice(0, V // 2))
-        round_result(1, res1, (0,))
+        round_result(nc.vector.tensor_copy, 1, res1, 0, P)
         result_planes(slice(V // 2, V))
 
         for q in range(4):

@@ -62,10 +62,6 @@ def tile_picked_zgcnii_relu_po_kernel(
         nc.gpsimd.memset(w2s_raw[:].bitcast(I32), 0)
         ident = keep.tile([P, P], F32, name="ident")
         make_identity(nc, ident[:])
-        for q in range(4):
-            nc.gpsimd.dma_start(
-                w2s_raw[32 * q : 32 * q + 4, :].bitcast(I32), w2_scales[0, 4 * q : 4 * q + 4, :].bitcast(I32)
-            )
 
         offs_sb = load_list("offs_sb", offs)
         w2w_raw = keep.tile([P, 2 * H], U8, name="w2w_raw", align_bytes=64)
@@ -78,12 +74,16 @@ def tile_picked_zgcnii_relu_po_kernel(
                 x_scales[:, 4 * q : 4 * q + 4, :].bitcast(I32),
             )
 
+        h = [keep.tile([P, S], F32, name=f"h{u}") for u in range(ROW_TILES)]
         w1_raw = {}
 
         def load_w1(g, u, tiles=1):
-            raw = keep.tile([P, PACK, tiles * P], F32, name=f"w1_raw{g}_{u}", align_bytes=64)
+            if (g, u) == (1, 1):
+                raw = h[0][:, 3 * P : 7 * P].rearrange("p (j c) -> p j c", j=PACK)
+            else:
+                raw = keep.tile([P, PACK, tiles * P], F32, name=f"w1_raw{g}_{u}", align_bytes=64)[:]
             rows = w1[g * P * PACK : (g + 1) * P * PACK, :].rearrange("(p j) c -> p j c", j=PACK)
-            nc.sync.dma_start(raw[:], rows[:, :, u * P : (u + tiles) * P])
+            nc.sync.dma_start(raw, rows[:, :, u * P : (u + tiles) * P])
             w1_raw[g, u] = raw
 
         turn_sb = keep.tile([P, PACK], F32, name="turn_sb")
@@ -99,6 +99,10 @@ def tile_picked_zgcnii_relu_po_kernel(
         load_w1(0, 1)
         load_w1(1, 1)
         load_w1(0, 2, 2)
+        for q in range(4):
+            nc.sync.dma_start(
+                w2s_raw[32 * q : 32 * q + 4, :].bitcast(I32), w2_scales[0, 4 * q : 4 * q + 4, :].bitcast(I32)
+            )
         pos_sb = [load_list("pos1_sb", pos1)]
         pos_sb.append(load_list("pos2_sb", pos2))
         cen_sb = load_list("cen_sb", cen)
@@ -130,11 +134,8 @@ def tile_picked_zgcnii_relu_po_kernel(
             scales = keep.tile([P, PASSES * cols], U8, name=f"w1_scales{u0}", align_bytes=64)
             for g in range(PASSES):
                 packed = grouped[:, g * cols * PACK : (g + 1) * cols * PACK].rearrange("p (c j) -> p c j", j=PACK)
-                dst, src = interleave(w1_raw[g, u0][:], packed)
-                if u0 == 1:
-                    nc.vector.tensor_copy(dst, src)
-                else:
-                    nc.scalar.copy(dst, src)
+                dst, src = interleave(w1_raw[g, u0], packed)
+                nc.scalar.copy(dst, src)
                 for k in range(tiles):
                     place = slice(g * cols + k * P, g * cols + (k + 1) * P)
                     w1_mx[g, u0 + k] = (codes[:, place], scales[:, place])
@@ -163,10 +164,8 @@ def tile_picked_zgcnii_relu_po_kernel(
                 scale=GATE_SCALE,
             )
 
-        h = []
-
         def hidden_rows(u):
-            h_u = keep.tile([P, S], F32, name=f"h{u}")
+            h_u = h[u]
             for lo, hi in FIRST_CUTS if u == 0 else BANK_CUTS:
                 cols = slice(lo, hi)
                 acc = psum_mx.tile([P, hi - lo], F32, name="acc")
@@ -182,7 +181,6 @@ def tile_picked_zgcnii_relu_po_kernel(
                         stop=(g == PASSES - 1),
                     )
                 nc.scalar.activation(h_u[:, cols], acc[:], RELU, scale=H_SCALE)
-            h.append(h_u)
 
         quantise_w1(1, 1, ring[:, SLOT - CAST : SLOT + CAST])
         hidden_rows(0)
@@ -191,7 +189,7 @@ def tile_picked_zgcnii_relu_po_kernel(
         w2w = keep.tile([P, PACK, P, 2], U8, name="w2w", align_bytes=64)
         nc.vector.tensor_copy(w2w[:], w2w_raw[:].rearrange("p (m t b) -> p t m b", t=PACK, b=2))
         w2s = keep.tile([P, PACK, P], U8, name="w2s", align_bytes=64)
-        nc.gpsimd.tensor_copy(w2s[:], w2s_raw[:].rearrange("p (m t) -> p t m", t=PACK))
+        nc.vector.tensor_copy(w2s[:], w2s_raw[:].rearrange("p (m t) -> p t m", t=PACK))
 
         z_stage = keep.tile([P, SLOT * PACK // 2], F32, name="z_stage", align_bytes=64)
         res_flat = keep.tile([P, V * PACK], BF16, name="res_bf", align_bytes=64)

@@ -25,20 +25,14 @@ PASSES = K // (P * PACK)
 BANK = 512
 LIST = 16
 ROW_TILES = H // P
-CHUNKS = ((0, 384), (384, 128))
-SLOT = CHUNKS[0][1]
-CAST = P * PACK // 2
+CHUNKS = ((0, 256), (256, 128), (384, 128))
 FIRST_CUTS = ((0, 512), (512, 768), (768, 1024))
 BANK_CUTS = ((0, 512), (512, 1024))
-RING = 4
+PAIRED = CHUNKS[1][0]
 H_SCALE = 0.6 * 0.1
 GATE_SCALE = 0.9 / 0.1
 Z_SCALE = 1.0 / 0.6
 Y_SCALE = 0.4
-
-
-def pieces(width):
-    return [(o, min(256, width - o)) for o in range(0, width, 256)]
 
 
 def tile_picked_zgcnii_relu_po_kernel(
@@ -48,8 +42,10 @@ def tile_picked_zgcnii_relu_po_kernel(
     with ExitStack() as ctx:
         lists = ctx.enter_context(tc.tile_pool(name="lists", bufs=1))
         keep = ctx.enter_context(tc.tile_pool(name="keep", bufs=1))
-        psum_mx = ctx.enter_context(tc.psum_pool(name="psum_mx", bufs=6))
-        psum_tr = ctx.enter_context(tc.psum_pool(name="psum_tr", bufs=1))
+        psum = ctx.enter_context(tc.psum_pool(name="psum", bufs=1))
+
+        def bank(k, shape):
+            return psum.tile(shape, F32, name=f"bank{k}")
 
         def load_list(name, src):
             held = lists.tile([P, src.shape[1]], U16, name=name)
@@ -57,11 +53,27 @@ def tile_picked_zgcnii_relu_po_kernel(
             return held
 
         xs_raw = keep.tile([P, T], U8, name="xs_raw", align_bytes=64)
-        nc.gpsimd.memset(xs_raw[:].bitcast(I32), 0)
+        nc.vector.memset(xs_raw[:].bitcast(I32), 0)
         w2s_raw = keep.tile([P, H], U8, name="w2s_raw", align_bytes=64)
-        nc.gpsimd.memset(w2s_raw[:].bitcast(I32), 0)
+        nc.vector.memset(w2s_raw[:].bitcast(I32), 0)
         ident = keep.tile([P, P], F32, name="ident")
         make_identity(nc, ident[:])
+
+        def load_words(g):
+            raw = keep.tile([P, T], I32, name=f"xw_raw{g}", align_bytes=64)
+            nc.sync.dma_start(raw[:], x_words[g].rearrange("p c r -> p (c r)").bitcast(I32))
+            return raw
+
+        h = [keep.tile([P, S], F32, name=f"h{u}") for u in range(ROW_TILES)]
+        w1_raw = {}
+
+        def load_w1(g, u0, tiles, raw):
+            rows = w1[g * P * PACK : (g + 1) * P * PACK, :].rearrange("(p j) c -> p j c", j=PACK)
+            nc.sync.dma_start(raw, rows[:, :, u0 * P : (u0 + tiles) * P])
+            w1_raw[g, u0] = raw
+
+        def own_raw(tag, tiles=1):
+            return keep.tile([P, PACK, tiles * P], F32, name=f"raw_{tag}", tag=tag, align_bytes=64)[:]
 
         offs_sb = load_list("offs_sb", offs)
         w2w_raw = keep.tile([P, 2 * H], U8, name="w2w_raw", align_bytes=64)
@@ -73,48 +85,23 @@ def tile_picked_zgcnii_relu_po_kernel(
                 xs_raw[32 * q : 32 * q + 4 * PASSES, :].bitcast(I32),
                 x_scales[:, 4 * q : 4 * q + 4, :].bitcast(I32),
             )
-
-        h = [keep.tile([P, S], F32, name=f"h{u}") for u in range(ROW_TILES)]
-        w1_raw = {}
-
-        def load_w1(g, u, tiles=1):
-            if (g, u) == (1, 1):
-                raw = h[0][:, 3 * P : 7 * P].rearrange("p (j c) -> p j c", j=PACK)
-            else:
-                raw = keep.tile([P, PACK, tiles * P], F32, name=f"w1_raw{g}_{u}", align_bytes=64)[:]
-            rows = w1[g * P * PACK : (g + 1) * P * PACK, :].rearrange("(p j) c -> p j c", j=PACK)
-            nc.sync.dma_start(raw, rows[:, :, u * P : (u + tiles) * P])
-            w1_raw[g, u] = raw
-
-        turn_sb = keep.tile([P, PACK], F32, name="turn_sb")
-
-        xw_raw = []
-        for g in range(PASSES):
-            raw = keep.tile([P, T], I32, name=f"xw_raw{g}", align_bytes=64)
-            nc.sync.dma_start(raw[:], x_words[g].rearrange("p c r -> p (c r)").bitcast(I32))
-            xw_raw.append(raw)
-            if g == 0:
-                load_w1(0, 0)
-                load_w1(1, 0)
-        load_w1(0, 1)
-        load_w1(1, 1)
-        load_w1(0, 2, 2)
+        xw_raw = [load_words(0)]
+        load_w1(0, 0, 1, own_raw("w1_00"))
+        load_w1(1, 0, 1, own_raw("w1_10"))
         for q in range(4):
             nc.sync.dma_start(
                 w2s_raw[32 * q : 32 * q + 4, :].bitcast(I32), w2_scales[0, 4 * q : 4 * q + 4, :].bitcast(I32)
             )
-        pos_sb = [load_list("pos1_sb", pos1)]
-        pos_sb.append(load_list("pos2_sb", pos2))
+        xw_raw.append(load_words(1))
+        pos_sb = [load_list("pos1_sb", pos1), load_list("pos2_sb", pos2)]
         cen_sb = load_list("cen_sb", cen)
-        load_w1(1, 2, 2)
+        load_w1(0, 1, 1, own_raw("w1_01"))
+        load_w1(1, 1, 1, own_raw("w1_11"))
         pos_sb.append(load_list("pos3_sb", pos3))
+        load_w1(0, 2, 2, own_raw("before_pairs", 2))
+        load_w1(1, 2, 2, own_raw("before_turned", 2))
+        turn_sb = keep.tile([P, PACK], F32, name="turn_sb")
         nc.sync.dma_start(turn_sb[:], turn.rearrange("(p t) o -> p (t o)", t=PACK))
-
-        ring = keep.tile([P, (1 + RING * D) * SLOT], F32, name="ring", align_bytes=64)
-
-        def ring_half(unit):
-            base = (1 + (unit % RING) * D) * SLOT
-            return ring[:, base : base + D * SLOT]
 
         turn_scaled = keep.tile([P, PACK], F32, name="turn_scaled")
         nc.scalar.activation(turn_scaled[:], turn_sb[:], COPY, scale=Y_SCALE)
@@ -127,9 +114,9 @@ def tile_picked_zgcnii_relu_po_kernel(
 
         w1_mx = {}
 
-        def quantise_w1(u0, tiles, staging):
+        def quantise_w1(u0, tiles, tag):
             cols = tiles * P
-            grouped = staging.bitcast(BF16)
+            grouped = keep.tile([P, PASSES * cols * PACK], BF16, name=f"w1_bf{u0}", tag=tag, align_bytes=64)
             codes = keep.tile([P, PASSES * cols], U32, name=f"w1_codes{u0}", align_bytes=64)
             scales = keep.tile([P, PASSES * cols], U8, name=f"w1_scales{u0}", align_bytes=64)
             for g in range(PASSES):
@@ -139,13 +126,13 @@ def tile_picked_zgcnii_relu_po_kernel(
                 for k in range(tiles):
                     place = slice(g * cols + k * P, g * cols + (k + 1) * P)
                     w1_mx[g, u0 + k] = (codes[:, place], scales[:, place])
-            nc.vector.quantize_mx(out=codes[:].bitcast(FP8X4), scales=scales[:], in_=grouped)
+            nc.vector.quantize_mx(out=codes[:].bitcast(FP8X4), scales=scales[:], in_=grouped[:])
 
+        xw = [keep.tile([P, S], U32, name=f"xw{g}", align_bytes=64) for g in range(PASSES)]
         xs = keep.tile([P, S], U8, name="xs", align_bytes=64)
         nc.vector.tensor_copy(xs[:], xs_raw[:].indirect(offs_sb[:]))
-        xw = [keep.tile([P, S], U32, name=f"xw{g}", align_bytes=64) for g in range(PASSES)]
         nc.vector.tensor_copy(xw[0][:], xw_raw[0][:].bitcast(U32).indirect(offs_sb[:]))
-        quantise_w1(0, 1, ring[:, 7 * SLOT - 2 * CAST : 7 * SLOT])
+        quantise_w1(0, 1, "w1_bf0")
         for lo, hi in FIRST_CUTS:
             nc.vector.tensor_copy(
                 xw[1][:, lo:hi], xw_raw[1][:].bitcast(U32).indirect(offs_sb[:, lo // LIST : hi // LIST])
@@ -154,7 +141,7 @@ def tile_picked_zgcnii_relu_po_kernel(
         gate_sb = [keep.tile([P, V], F32, name=f"gate{d}") for d in range(D)]
 
         for d in range(D):
-            spread = psum_mx.tile([P, PACK, P], F32, name="acc")
+            spread = bank(d, [P, PACK, P])
             for b in range(PACK):
                 nc.tensor.transpose(spread[:, b, :], gate_cols[:, d, b : b + 1].to_broadcast([P, P]), ident[:])
             nc.scalar.activation(
@@ -166,9 +153,9 @@ def tile_picked_zgcnii_relu_po_kernel(
 
         def hidden_rows(u):
             h_u = h[u]
-            for lo, hi in FIRST_CUTS if u == 0 else BANK_CUTS:
+            for k, (lo, hi) in enumerate(FIRST_CUTS if u == 0 else BANK_CUTS):
                 cols = slice(lo, hi)
-                acc = psum_mx.tile([P, hi - lo], F32, name="acc")
+                acc = bank((3 + k, k, 2 + k, 4 + k)[u], [P, hi - lo])
                 for g in range(PASSES):
                     codes, scales = w1_mx[g, u]
                     nc.tensor.matmul_mx(
@@ -182,8 +169,8 @@ def tile_picked_zgcnii_relu_po_kernel(
                     )
                 nc.scalar.activation(h_u[:, cols], acc[:], RELU, scale=H_SCALE)
 
-        quantise_w1(1, 1, ring[:, SLOT - CAST : SLOT + CAST])
         hidden_rows(0)
+        quantise_w1(1, 1, "before_term0_1")
         hidden_rows(1)
 
         w2w = keep.tile([P, PACK, P, 2], U8, name="w2w", align_bytes=64)
@@ -191,7 +178,10 @@ def tile_picked_zgcnii_relu_po_kernel(
         w2s = keep.tile([P, PACK, P], U8, name="w2s", align_bytes=64)
         nc.vector.tensor_copy(w2s[:], w2s_raw[:].rearrange("p (m t) -> p t m", t=PACK))
 
-        z_stage = keep.tile([P, SLOT * PACK // 2], F32, name="z_stage", align_bytes=64)
+        quantise_w1(2, 2, "before_term1_1")
+        hidden_rows(2)
+        hidden_rows(3)
+
         res_flat = keep.tile([P, V * PACK], BF16, name="res_bf", align_bytes=64)
         res_bf = res_flat[:].rearrange("p (c t) -> p c t", t=PACK)
         out_codes = keep.tile([P, V], U32, name="out_codes", align_bytes=64)
@@ -199,110 +189,130 @@ def tile_picked_zgcnii_relu_po_kernel(
         out_rows = out_0.rearrange("(p t) v -> p t v", t=PACK)
         out_words = out_1[0].rearrange("p c r -> p (c r)").bitcast(I32)
 
-        def mix(n):
-            c0, width = CHUNKS[n]
+        z_all = keep.tile([P, PACK * V], F32, name="z_turned", tag="before_turned", align_bytes=64)
+        z_turned = z_all[:].rearrange("v (b t p) -> v b t p", t=PACK, p=P)
+
+        z_pairs = keep.tile([P, (V - PAIRED) * 2], F32, name="z_pairs", tag="before_pairs", align_bytes=64)
+        z_pairs_bf = z_pairs[:].bitcast(BF16).rearrange("v (b w p e) -> v b w p e", w=2, p=P, e=2)
+
+        def mix(u, c0, width, slot, turned):
             blocks = width // P
             lcols = slice(c0 // LIST, (c0 + width) // LIST)
             cols = slice(c0, c0 + width)
-            z_flat = keep.tile([P, PACK * width], F32, name=f"z_turned{n}")
-            z_turned = z_flat[:].rearrange("v (b t p) -> v b t p", t=PACK, p=P)
-            for u in range(ROW_TILES):
-                if n == 0:
-                    slot = [ring[:, 0:SLOT]] + [ring_half(u)[:, k * SLOT : (k + 1) * SLOT] for k in ((0, 2, 1), (0, 1, 2))[u % 2]]
-                elif u + 1 < ROW_TILES:
-                    places = [ring[:, 0:SLOT]] + [ring_half(2)[:, k * SLOT : (k + 1) * SLOT] for k in range(D)]
-                    slot = [places[k][:, u * width : (u + 1) * width] for k in range(D + 1)]
-                else:
-                    slot = [z_stage[:, (k + 2) * width : (k + 3) * width] for k in range(D + 1)]
-                if n == 0:
-                    turned = psum_tr.tile([P, width], F32, name=f"turned{u % 2}")[:]
-                elif u == 0:
-                    early = psum_tr.tile([P, (ROW_TILES - 1) * width], F32, name="turned1")
-                if n == 1:
-                    if u + 1 < ROW_TILES:
-                        turned = early[:, u * width : (u + 1) * width]
-                    else:
-                        turned = psum_tr.tile([P, width], F32, name="turned0")[:]
 
-                def add_turned(term, first, final):
-                    for b in range(blocks):
-                        nc.tensor.matmul(
-                            turned[:, b * P : (b + 1) * P],
-                            term[:, b * P : (b + 1) * P],
-                            ident[:],
-                            start=(first and b == 0),
-                            stop=(final and b == blocks - 1),
-                            is_transpose=True,
-                        )
-
-                window = h[u][:]
-                nc.vector.tensor_tensor(slot[0], window.indirect(pos_sb[0][:, lcols]), gate_sb[0][:, cols], MULT)
-                nc.vector.tensor_tensor(slot[1], window.indirect(pos_sb[1][:, lcols]), gate_sb[1][:, cols], MULT)
-                nc.vector.tensor_tensor(slot[3], window.indirect(cen_sb[:, lcols]), slot[0], ADD)
-                add_turned(slot[3], True, False)
-                add_turned(slot[1], False, False)
-                if n == 0 and u == 0:
-                    quantise_w1(2, 2, ring[:, 4 * SLOT - P : 4 * SLOT - P + 4 * CAST])
-                    hidden_rows(2)
-                    hidden_rows(3)
-                nc.vector.tensor_tensor(slot[2], window.indirect(pos_sb[2][:, lcols]), gate_sb[2][:, cols], MULT)
-                add_turned(slot[2], False, True)
-                if n == 0 or u + 1 == ROW_TILES:
-                    nc.scalar.copy(
-                        z_turned[:, :, :, u * 32 : (u + 1) * 32],
-                        turned.rearrange("v (b q t) -> v b t q", t=PACK, q=32),
+            def add_turned(term, first, final):
+                for b in range(blocks):
+                    nc.tensor.matmul(
+                        turned[:, b * P : (b + 1) * P],
+                        term[:, b * P : (b + 1) * P],
+                        ident[:],
+                        start=(first and b == 0),
+                        stop=(final and b == blocks - 1),
+                        is_transpose=True,
                     )
-                elif u + 2 == ROW_TILES:
-                    nc.scalar.copy(
-                        z_turned[:, 0, :, 0 : (u + 1) * 32], early[:].rearrange("v (q t) -> v t q", t=PACK)
-                    )
-            return z_flat
 
-        def quantise_z(n, z_flat):
-            c0, width = CHUNKS[n]
-            z_turned = z_flat[:].rearrange("v (b t p) -> v b t p", t=PACK, p=P)
-            zs = z_flat[:].rearrange("p (t v) -> p t v", t=PACK)
-            if n == 0:
-                z_bf = z_stage[:].bitcast(BF16).rearrange("p (c t) -> p c t", t=PACK)
+            window = h[u][:]
+            nc.vector.tensor_tensor(slot[0], window.indirect(pos_sb[0][:, lcols]), gate_sb[0][:, cols], MULT)
+            nc.vector.tensor_tensor(slot[1], window.indirect(pos_sb[1][:, lcols]), gate_sb[1][:, cols], MULT)
+            nc.vector.tensor_tensor(slot[3], window.indirect(cen_sb[:, lcols]), slot[0], ADD)
+            nc.vector.tensor_tensor(slot[2], window.indirect(pos_sb[2][:, lcols]), gate_sb[2][:, cols], MULT)
+            order = (1, 3, 2)
+            for k in order:
+                add_turned(slot[k], k == order[0], k == order[2])
+            rows = slice(u * 32, (u + 1) * 32)
+            lo = max(c0, PAIRED)
+            for b in range(lo // P, c0 // P + blocks):
+                nc.scalar.activation(
+                    z_pairs_bf[:, b - PAIRED // P, :, rows, :],
+                    turned[:, b * P - c0 : (b + 1) * P - c0].rearrange("v (q w e) -> v w q e", w=2, e=2),
+                    COPY,
+                    scale=Z_SCALE,
+                )
+            nc.scalar.copy(
+                z_turned[:, c0 // P : c0 // P + blocks, :, rows],
+                turned.rearrange("v (b q t) -> v b t q", t=PACK, q=32),
+            )
+
+        def term_slots(name, tag, count, width):
+            terms = keep.tile([P, count * width], F32, name=name, tag=tag, align_bytes=64)
+            return [terms[:, k * width : (k + 1) * width] for k in range(count)]
+
+        def mix_unit(step, u, c0, width, tag):
+            if u < 2:
+                slot = term_slots(f"first{u}", f"before_term{u}_0", 1, width) + term_slots(f"rest{u}", f"before_term{u}_1", D, width)
             else:
-                z_bf = res_bf[:, P // 2 : P // 2 + width, :]
+                slot = term_slots(f"terms{step}", tag, D + 1, width)
+            mix(u, c0, width, slot, bank((6, 7, 6, 7, 7, 0)[step], [P, width])[:])
+
+        def quantise_z(n, tag):
+            c0, width = CHUNKS[n]
+            zs = keep.tile([P, PACK, width], F32, name=f"z_scaled{n}")
+            z_flat = keep.tile([P, PACK * width], BF16, name=f"z_bf{n}", tag=tag, align_bytes=64)
+            z_bf = z_flat[:].rearrange("p (c t) -> p c t", t=PACK)
             z_codes = keep.tile([P, width], U32, name=f"z_codes{n}", align_bytes=64)
             z_scales = keep.tile([P, width], U8, name=f"z_scales{n}", align_bytes=64)
             backs = []
             for b in range(width // P):
-                back = psum_mx.tile([P, PACK, P], F32, name="acc")
+                back = bank(b, [P, PACK, P])
                 for t in range(PACK):
-                    nc.tensor.transpose(back[:, t, :], z_turned[:, b, t, :], ident[:])
+                    nc.tensor.transpose(back[:, t, :], z_turned[:, c0 // P + b, t, :], ident[:])
                 nc.scalar.activation(
                     z_bf[:, b * P : (b + 1) * P, :], back[:].rearrange("p t v -> p v t"), COPY, scale=Z_SCALE
                 )
                 backs.append(back)
-            for o, w in pieces(width):
-                nc.vector.quantize_mx(
-                    out=z_codes[:, o : o + w].bitcast(FP8X4),
-                    scales=z_scales[:, o : o + w],
-                    in_=z_bf[:, o : o + w, :].rearrange("p c t -> p (c t)"),
-                )
+            nc.vector.quantize_mx(out=z_codes[:].bitcast(FP8X4), scales=z_scales[:], in_=z_flat[:])
+            return zs, backs, z_codes, z_scales
+
+        def keep_z(zs, backs):
             for b, back in enumerate(backs):
                 nc.scalar.copy(zs[:, :, b * P : (b + 1) * P], back[:])
-            return zs, z_codes, z_scales
+
+        def quantise_pairs(n):
+            c0, width = CHUNKS[n]
+            z_words = keep.tile([P, 2 * width], F32, name=f"z_words{n}", align_bytes=64)
+            z_codes = keep.tile([P, width], U32, name=f"z_codes{n}", align_bytes=64)
+            z_scales = keep.tile([P, width], U8, name=f"z_scales{n}", align_bytes=64)
+            pairs = bank(3 + n, [P, width // P, 2, P])
+            for b in range(width // P):
+                for w in range(2):
+                    place = ((c0 - PAIRED) * 2) + (b * 2 + w) * P
+                    nc.tensor.transpose(pairs[:, b, w, :], z_pairs[:, place : place + P], ident[:])
+            nc.scalar.copy(
+                z_words[:].rearrange("p (b v w) -> p b v w", w=2, v=P), pairs[:].rearrange("p b w v -> p b v w")
+            )
+            nc.vector.quantize_mx(out=z_codes[:].bitcast(FP8X4), scales=z_scales[:], in_=z_words[:].bitcast(BF16))
+            return z_codes, z_scales
+
+        def turn_back(n):
+            c0, width = CHUNKS[n]
+            zs = keep.tile([P, PACK, width], F32, name=f"z_scaled{n}")
+            for b in range(width // P):
+                back = bank((0, 1, 0)[n], [P, PACK, P])
+                for t in range(PACK):
+                    nc.tensor.transpose(back[:, t, :], z_turned[:, c0 // P + b, t, :], ident[:])
+                nc.scalar.copy(zs[:, :, b * P : (b + 1) * P], back[:])
+            return zs
 
         def second_product(n, z_codes, z_scales):
             width = CHUNKS[n][1]
             banks = []
             for t in range(PACK):
-                y = psum_mx.tile([P, BANK], F32, name="acc")
-                for o, w in pieces(width):
-                    nc.tensor.matmul_mx(
-                        out=y[:, o : o + w],
-                        lhsT=w2w[:, t, :, :].rearrange("p m b -> p (m b)").bitcast(FP4X4),
-                        lhsT_scale=w2s[:, t, :],
-                        rhs=z_codes[:, o : o + w].bitcast(FP8X4),
-                        rhs_scale=z_scales[:, o : o + w],
-                        start=True,
-                        stop=True,
-                    )
-                banks.append(y)
+                if n == 1:
+                    y = bank((6, 7, 2, 3)[t], [P, width])
+                else:
+                    if t % 2 == 0:
+                        both = bank(((2, 3), None, (4, 5))[n][t // 2], [P, 2, width])
+                    y = both[:, t % 2, :]
+                nc.tensor.matmul_mx(
+                    out=y[:],
+                    lhsT=w2w[:, t, :, :].rearrange("p m b -> p (m b)").bitcast(FP4X4),
+                    lhsT_scale=w2s[:, t, :],
+                    rhs=z_codes[:].bitcast(FP8X4),
+                    rhs_scale=z_scales[:],
+                    start=True,
+                    stop=True,
+                )
+                banks.append(y[:])
             return banks
 
         def combine(n, zs, banks):
@@ -310,7 +320,7 @@ def tile_picked_zgcnii_relu_po_kernel(
             res = keep.tile([P, PACK, width], F32, name=f"res{n}")
             for t, y in enumerate(banks):
                 nc.vector.scalar_tensor_tensor(
-                    res[:, t, :], y[:, 0:width], turn_scaled[:, t : t + 1], zs[:, t, :], MULT, ADD
+                    res[:, t, :], y, turn_scaled[:, t : t + 1], zs[:, t, :], MULT, ADD
                 )
             nc.sync.dma_start(out_rows[:, :, c0 : c0 + width], res[:])
             return res
@@ -328,16 +338,27 @@ def tile_picked_zgcnii_relu_po_kernel(
             )
             nc.sync.dma_start(out_words[:, cols], out_codes[:, cols].bitcast(I32))
 
-        zs0, z_codes0, z_scales0 = quantise_z(0, mix(0))
-        banks0 = second_product(0, z_codes0, z_scales0)
-        turned1 = mix(1)
-        res0 = combine(0, zs0, banks0)
-        zs1, z_codes1, z_scales1 = quantise_z(1, turned1)
+        mix_unit(0, 0, 0, V, None)
+        mix_unit(1, 1, 0, V, None)
+        mix_unit(2, 2, *CHUNKS[0], "before_terms2")
+        mix_unit(3, 3, *CHUNKS[0], "terms3")
+        zs0, backs0, z_codes0, z_scales0 = quantise_z(0, "z_bf0")
+        mix_unit(4, 2, PAIRED, V - PAIRED, "terms4")
+        keep_z(zs0, backs0)
+        mix_unit(5, 3, PAIRED, V - PAIRED, "terms5")
+        planes1 = quantise_pairs(1)
+        planes2 = quantise_pairs(2)
+        res0 = combine(0, zs0, second_product(0, z_codes0, z_scales0))
+        zs1 = turn_back(1)
+        zs2 = turn_back(2)
         round_result(nc.vector.tensor_copy, 0, res0, 0, P)
-        round_result(nc.scalar.copy, 0, res0, P, SLOT)
-        res1 = combine(1, zs1, second_product(1, z_codes1, z_scales1))
+        round_result(nc.vector.tensor_copy, 0, res0, P, 2 * P)
         result_planes(slice(0, V // 2))
-        round_result(nc.vector.tensor_copy, 1, res1, 0, P)
+        banks1 = second_product(1, *planes1)
+        res1 = combine(1, zs1, banks1)
+        res2 = combine(2, zs2, second_product(2, *planes2))
+        round_result(nc.scalar.copy, 1, res1, 0, P)
+        round_result(nc.vector.tensor_copy, 2, res2, 0, P)
         result_planes(slice(V // 2, V))
 
         for q in range(4):

@@ -27,7 +27,6 @@ LIST = 16
 ROW_TILES = H // P
 CHUNKS = ((0, 256), (256, 128), (384, 128))
 FIRST_CUTS = ((0, 512), (512, 768), (768, 1024))
-BANK_CUTS = ((0, 512), (512, 1024))
 PAIRED = CHUNKS[1][0]
 H_SCALE = 0.6 * 0.1
 GATE_SCALE = 0.9 / 0.1
@@ -53,9 +52,9 @@ def tile_picked_zgcnii_relu_po_kernel(
             return held
 
         xs_raw = keep.tile([P, T], U8, name="xs_raw", align_bytes=64)
-        nc.vector.memset(xs_raw[:].bitcast(I32), 0)
+        nc.gpsimd.memset(xs_raw[:].bitcast(I32), 0)
         w2s_raw = keep.tile([P, H], U8, name="w2s_raw", align_bytes=64)
-        nc.vector.memset(w2s_raw[:].bitcast(I32), 0)
+        nc.gpsimd.memset(w2s_raw[:].bitcast(I32), 0)
         ident = keep.tile([P, P], F32, name="ident")
         make_identity(nc, ident[:])
 
@@ -87,19 +86,19 @@ def tile_picked_zgcnii_relu_po_kernel(
             )
         xw_raw = [load_words(0)]
         load_w1(0, 0, 1, own_raw("w1_00"))
-        load_w1(1, 0, 1, own_raw("w1_10"))
         for q in range(4):
             nc.sync.dma_start(
                 w2s_raw[32 * q : 32 * q + 4, :].bitcast(I32), w2_scales[0, 4 * q : 4 * q + 4, :].bitcast(I32)
             )
         xw_raw.append(load_words(1))
+        load_w1(1, 0, 1, own_raw("before_last_words"))
+        load_w1(0, 1, 1, h[0][:, 3 * P : 7 * P].rearrange("p (j c) -> p j c", j=PACK))
+        load_w1(1, 1, 1, own_raw("w1_11"))
         pos_sb = [load_list("pos1_sb", pos1), load_list("pos2_sb", pos2)]
         cen_sb = load_list("cen_sb", cen)
-        load_w1(0, 1, 1, own_raw("w1_01"))
-        load_w1(1, 1, 1, own_raw("w1_11"))
         pos_sb.append(load_list("pos3_sb", pos3))
         load_w1(0, 2, 2, own_raw("before_pairs", 2))
-        load_w1(1, 2, 2, own_raw("before_turned", 2))
+        load_w1(1, 2, 2, own_raw("before_term1_1", 2))
         turn_sb = keep.tile([P, PACK], F32, name="turn_sb")
         nc.sync.dma_start(turn_sb[:], turn.rearrange("(p t) o -> p (t o)", t=PACK))
 
@@ -114,28 +113,42 @@ def tile_picked_zgcnii_relu_po_kernel(
 
         w1_mx = {}
 
-        def quantise_w1(u0, tiles, tag):
+        def quantise_w1(u0, tiles, tag, passes=(0, 1)):
             cols = tiles * P
-            grouped = keep.tile([P, PASSES * cols * PACK], BF16, name=f"w1_bf{u0}", tag=tag, align_bytes=64)
-            codes = keep.tile([P, PASSES * cols], U32, name=f"w1_codes{u0}", align_bytes=64)
-            scales = keep.tile([P, PASSES * cols], U8, name=f"w1_scales{u0}", align_bytes=64)
-            for g in range(PASSES):
-                packed = grouped[:, g * cols * PACK : (g + 1) * cols * PACK].rearrange("p (c j) -> p c j", j=PACK)
+            count = len(passes)
+            grouped = keep.tile([P, count * cols * PACK], BF16, name=tag + "_bf", tag=tag, align_bytes=64)
+            codes = keep.tile([P, count * cols], U32, name=tag + "_codes", align_bytes=64)
+            scales = keep.tile([P, count * cols], U8, name=tag + "_scales", align_bytes=64)
+            for n, g in enumerate(passes):
+                packed = grouped[:, n * cols * PACK : (n + 1) * cols * PACK].rearrange("p (c j) -> p c j", j=PACK)
                 dst, src = interleave(w1_raw[g, u0], packed)
-                nc.scalar.copy(dst, src)
+                if (g, u0) == (1, 1):
+                    nc.vector.tensor_copy(dst, src)
+                else:
+                    nc.scalar.copy(dst, src)
                 for k in range(tiles):
-                    place = slice(g * cols + k * P, g * cols + (k + 1) * P)
+                    place = slice(n * cols + k * P, n * cols + (k + 1) * P)
                     w1_mx[g, u0 + k] = (codes[:, place], scales[:, place])
             nc.vector.quantize_mx(out=codes[:].bitcast(FP8X4), scales=scales[:], in_=grouped[:])
 
-        xw = [keep.tile([P, S], U32, name=f"xw{g}", align_bytes=64) for g in range(PASSES)]
         xs = keep.tile([P, S], U8, name="xs", align_bytes=64)
         nc.vector.tensor_copy(xs[:], xs_raw[:].indirect(offs_sb[:]))
-        nc.vector.tensor_copy(xw[0][:], xw_raw[0][:].bitcast(U32).indirect(offs_sb[:]))
-        quantise_w1(0, 1, "w1_bf0")
+        xw0 = keep.tile([P, S], U32, name="xw0", align_bytes=64)
+        nc.vector.tensor_copy(xw0[:], xw_raw[0][:].bitcast(U32).indirect(offs_sb[:]))
+        quantise_w1(0, 1, "w1_bf00", (0,))
+        quantise_w1(0, 1, "w1_bf10", (1,))
+        last_lo = FIRST_CUTS[-1][0]
+        xw1 = keep.tile([P, last_lo], U32, name="xw1", align_bytes=64)
+        xw1_last = keep.tile([P, S - last_lo], U32, name="xw1_last", tag="before_last_words", align_bytes=64)
+
+        def words(g, lo, hi):
+            if g == 0:
+                return xw0[:, lo:hi]
+            return xw1[:, lo:hi] if hi <= last_lo else xw1_last[:, lo - last_lo : hi - last_lo]
+
         for lo, hi in FIRST_CUTS:
             nc.vector.tensor_copy(
-                xw[1][:, lo:hi], xw_raw[1][:].bitcast(U32).indirect(offs_sb[:, lo // LIST : hi // LIST])
+                words(1, lo, hi), xw_raw[1][:].bitcast(U32).indirect(offs_sb[:, lo // LIST : hi // LIST])
             )
 
         gate_sb = [keep.tile([P, V], F32, name=f"gate{d}") for d in range(D)]
@@ -153,32 +166,32 @@ def tile_picked_zgcnii_relu_po_kernel(
 
         def hidden_rows(u):
             h_u = h[u]
-            for k, (lo, hi) in enumerate(FIRST_CUTS if u == 0 else BANK_CUTS):
+            for k, (lo, hi) in enumerate(FIRST_CUTS):
                 cols = slice(lo, hi)
-                acc = bank((3 + k, k, 2 + k, 4 + k)[u], [P, hi - lo])
+                acc = bank(3 * ((u + 1) % 2) + k, [P, hi - lo])
                 for g in range(PASSES):
                     codes, scales = w1_mx[g, u]
                     nc.tensor.matmul_mx(
                         out=acc[:],
                         lhsT=codes.bitcast(FP8X4),
                         lhsT_scale=scales,
-                        rhs=xw[g][:, cols].bitcast(FP8X4),
+                        rhs=words(g, lo, hi).bitcast(FP8X4),
                         rhs_scale=xs[4 * g : P, cols],
                         start=(g == 0),
                         stop=(g == PASSES - 1),
                     )
                 nc.scalar.activation(h_u[:, cols], acc[:], RELU, scale=H_SCALE)
 
+        quantise_w1(1, 1, "before_term0_0")
         hidden_rows(0)
-        quantise_w1(1, 1, "before_term0_1")
         hidden_rows(1)
 
         w2w = keep.tile([P, PACK, P, 2], U8, name="w2w", align_bytes=64)
         nc.vector.tensor_copy(w2w[:], w2w_raw[:].rearrange("p (m t b) -> p t m b", t=PACK, b=2))
         w2s = keep.tile([P, PACK, P], U8, name="w2s", align_bytes=64)
-        nc.vector.tensor_copy(w2s[:], w2s_raw[:].rearrange("p (m t) -> p t m", t=PACK))
+        nc.gpsimd.tensor_copy(w2s[:], w2s_raw[:].rearrange("p (m t) -> p t m", t=PACK))
 
-        quantise_w1(2, 2, "before_term1_1")
+        quantise_w1(2, 2, "w1_bf2")
         hidden_rows(2)
         hidden_rows(3)
 
@@ -189,7 +202,7 @@ def tile_picked_zgcnii_relu_po_kernel(
         out_rows = out_0.rearrange("(p t) v -> p t v", t=PACK)
         out_words = out_1[0].rearrange("p c r -> p (c r)").bitcast(I32)
 
-        z_all = keep.tile([P, PACK * V], F32, name="z_turned", tag="before_turned", align_bytes=64)
+        z_all = keep.tile([P, PACK * V], F32, name="z_turned", align_bytes=64)
         z_turned = z_all[:].rearrange("v (b t p) -> v b t p", t=PACK, p=P)
 
         z_pairs = keep.tile([P, (V - PAIRED) * 2], F32, name="z_pairs", tag="before_pairs", align_bytes=64)
@@ -285,7 +298,10 @@ def tile_picked_zgcnii_relu_po_kernel(
 
         def turn_back(n):
             c0, width = CHUNKS[n]
-            zs = keep.tile([P, PACK, width], F32, name=f"z_scaled{n}")
+            if n == 1:
+                zs = res_flat[:].bitcast(F32)[:, 2 * P : 6 * P].rearrange("p (t v) -> p t v", t=PACK)
+            else:
+                zs = keep.tile([P, PACK, width], F32, name=f"z_scaled{n}")
             for b in range(width // P):
                 back = bank((0, 1, 0)[n], [P, PACK, P])
                 for t in range(PACK):
@@ -297,11 +313,11 @@ def tile_picked_zgcnii_relu_po_kernel(
             width = CHUNKS[n][1]
             banks = []
             for t in range(PACK):
-                if n == 1:
+                if n < 2:
                     y = bank((6, 7, 2, 3)[t], [P, width])
                 else:
                     if t % 2 == 0:
-                        both = bank(((2, 3), None, (4, 5))[n][t // 2], [P, 2, width])
+                        both = bank(4 + t // 2, [P, 2, width])
                     y = both[:, t % 2, :]
                 nc.tensor.matmul_mx(
                     out=y[:],
@@ -352,12 +368,12 @@ def tile_picked_zgcnii_relu_po_kernel(
         zs1 = turn_back(1)
         zs2 = turn_back(2)
         round_result(nc.vector.tensor_copy, 0, res0, 0, P)
-        round_result(nc.vector.tensor_copy, 0, res0, P, 2 * P)
-        result_planes(slice(0, V // 2))
         banks1 = second_product(1, *planes1)
         res1 = combine(1, zs1, banks1)
         res2 = combine(2, zs2, second_product(2, *planes2))
+        round_result(nc.scalar.copy, 0, res0, P, 2 * P)
         round_result(nc.scalar.copy, 1, res1, 0, P)
+        result_planes(slice(0, V // 2))
         round_result(nc.vector.tensor_copy, 2, res2, 0, P)
         result_planes(slice(V // 2, V))
 

@@ -28,6 +28,7 @@ ROW_TILES = H // P
 CHUNKS = ((0, 256), (256, 128), (384, 128))
 FIRST_CUTS = ((0, 512), (512, 768), (768, 1024))
 PAIRED = CHUNKS[1][0]
+QUARTER_CUTS = tuple((lo, lo + 256) for lo in range(0, S, 256))
 H_SCALE = 0.6 * 0.1
 GATE_SCALE = 0.9 / 0.1
 Z_SCALE = 1.0 / 0.6
@@ -92,12 +93,12 @@ def tile_picked_zgcnii_relu_po_kernel(
             )
         xw_raw.append(load_words(1))
         load_w1(1, 0, 1, own_raw("before_last_words"))
-        load_w1(0, 1, 1, h[0][:, 3 * P : 7 * P].rearrange("p (j c) -> p j c", j=PACK))
+        load_w1(0, 1, 1, h[0][:].rearrange("p (j c) -> p j c", j=PACK)[:, :, 0:P])
         load_w1(1, 1, 1, own_raw("w1_11"))
         pos_sb = [load_list("pos1_sb", pos1), load_list("pos2_sb", pos2)]
         cen_sb = load_list("cen_sb", cen)
         pos_sb.append(load_list("pos3_sb", pos3))
-        load_w1(0, 2, 2, own_raw("before_pairs", 2))
+        load_w1(0, 2, 2, h[1][:].rearrange("p (j c) -> p j c", j=PACK))
         load_w1(1, 2, 2, own_raw("before_term1_1", 2))
         turn_sb = keep.tile([P, PACK], F32, name="turn_sb")
         nc.sync.dma_start(turn_sb[:], turn.rearrange("(p t) o -> p (t o)", t=PACK))
@@ -166,9 +167,9 @@ def tile_picked_zgcnii_relu_po_kernel(
 
         def hidden_rows(u):
             h_u = h[u]
-            for k, (lo, hi) in enumerate(FIRST_CUTS):
+            for k, (lo, hi) in enumerate(QUARTER_CUTS if u == 0 else FIRST_CUTS):
                 cols = slice(lo, hi)
-                acc = bank(3 * ((u + 1) % 2) + k, [P, hi - lo])
+                acc = bank(((3, 4, 5, 7), (0, 1, 2), (3, 4, 5), (0, 1, 2))[u][k], [P, hi - lo])
                 for g in range(PASSES):
                     codes, scales = w1_mx[g, u]
                     nc.tensor.matmul_mx(
@@ -184,6 +185,7 @@ def tile_picked_zgcnii_relu_po_kernel(
 
         quantise_w1(1, 1, "before_term0_0")
         hidden_rows(0)
+        quantise_w1(2, 2, "w1_bf2")
         hidden_rows(1)
 
         w2w = keep.tile([P, PACK, P, 2], U8, name="w2w", align_bytes=64)
@@ -191,7 +193,6 @@ def tile_picked_zgcnii_relu_po_kernel(
         w2s = keep.tile([P, PACK, P], U8, name="w2s", align_bytes=64)
         nc.gpsimd.tensor_copy(w2s[:], w2s_raw[:].rearrange("p (m t) -> p t m", t=PACK))
 
-        quantise_w1(2, 2, "w1_bf2")
         hidden_rows(2)
         hidden_rows(3)
 
@@ -202,11 +203,12 @@ def tile_picked_zgcnii_relu_po_kernel(
         out_rows = out_0.rearrange("(p t) v -> p t v", t=PACK)
         out_words = out_1[0].rearrange("p c r -> p (c r)").bitcast(I32)
 
-        z_all = keep.tile([P, PACK * V], F32, name="z_turned", align_bytes=64)
-        z_turned = z_all[:].rearrange("v (b t p) -> v b t p", t=PACK, p=P)
+        z_both = keep.tile([P, PACK * V + (V - PAIRED) * 2], F32, name="z_both", tag="w1_bf2", align_bytes=64)
+        z_all = z_both[:, 0 : PACK * V]
+        z_turned = z_all.rearrange("v (b t p) -> v b t p", t=PACK, p=P)
 
-        z_pairs = keep.tile([P, (V - PAIRED) * 2], F32, name="z_pairs", tag="before_pairs", align_bytes=64)
-        z_pairs_bf = z_pairs[:].bitcast(BF16).rearrange("v (b w p e) -> v b w p e", w=2, p=P, e=2)
+        z_pairs = z_both[:, PACK * V :]
+        z_pairs_bf = z_pairs.bitcast(BF16).rearrange("v (b w p e) -> v b w p e", w=2, p=P, e=2)
 
         def mix(u, c0, width, slot, turned):
             blocks = width // P
@@ -251,10 +253,7 @@ def tile_picked_zgcnii_relu_po_kernel(
             return [terms[:, k * width : (k + 1) * width] for k in range(count)]
 
         def mix_unit(step, u, c0, width, tag):
-            if u < 2:
-                slot = term_slots(f"first{u}", f"before_term{u}_0", 1, width) + term_slots(f"rest{u}", f"before_term{u}_1", D, width)
-            else:
-                slot = term_slots(f"terms{step}", tag, D + 1, width)
+            slot = term_slots(f"terms{step}", tag, D + 1, width)
             mix(u, c0, width, slot, bank((6, 7, 6, 7, 7, 0)[step], [P, width])[:])
 
         def quantise_z(n, tag):
@@ -298,10 +297,7 @@ def tile_picked_zgcnii_relu_po_kernel(
 
         def turn_back(n):
             c0, width = CHUNKS[n]
-            if n == 1:
-                zs = res_flat[:].bitcast(F32)[:, 2 * P : 6 * P].rearrange("p (t v) -> p t v", t=PACK)
-            else:
-                zs = keep.tile([P, PACK, width], F32, name=f"z_scaled{n}")
+            zs = keep.tile([P, PACK, width], F32, name=f"z_scaled{n}")
             for b in range(width // P):
                 back = bank((0, 1, 0)[n], [P, PACK, P])
                 for t in range(PACK):
@@ -354,8 +350,8 @@ def tile_picked_zgcnii_relu_po_kernel(
             )
             nc.sync.dma_start(out_words[:, cols], out_codes[:, cols].bitcast(I32))
 
-        mix_unit(0, 0, 0, V, None)
-        mix_unit(1, 1, 0, V, None)
+        mix_unit(0, 0, 0, V, "before_term0_0")
+        mix_unit(1, 1, 0, V, "before_term1_1")
         mix_unit(2, 2, *CHUNKS[0], "before_terms2")
         mix_unit(3, 3, *CHUNKS[0], "terms3")
         zs0, backs0, z_codes0, z_scales0 = quantise_z(0, "z_bf0")
@@ -368,14 +364,14 @@ def tile_picked_zgcnii_relu_po_kernel(
         zs1 = turn_back(1)
         zs2 = turn_back(2)
         round_result(nc.vector.tensor_copy, 0, res0, 0, P)
-        banks1 = second_product(1, *planes1)
-        res1 = combine(1, zs1, banks1)
+        round_result(nc.vector.tensor_copy, 0, res0, P, 2 * P)
+        result_planes(slice(0, 2 * P))
+        res1 = combine(1, zs1, second_product(1, *planes1))
         res2 = combine(2, zs2, second_product(2, *planes2))
-        round_result(nc.scalar.copy, 0, res0, P, 2 * P)
         round_result(nc.scalar.copy, 1, res1, 0, P)
-        result_planes(slice(0, V // 2))
         round_result(nc.vector.tensor_copy, 2, res2, 0, P)
-        result_planes(slice(V // 2, V))
+        result_planes(slice(2 * P, 3 * P))
+        result_planes(slice(3 * P, V))
 
         for q in range(4):
             queue = nc.sync if q % 2 == 0 else nc.scalar

@@ -229,11 +229,11 @@ def tile_picked_zgcnii_relu_po_kernel(
             window = h[u][:]
             nc.vector.tensor_tensor(slot[0], window.indirect(pos_sb[0][:, lcols]), gate_sb[0][:, cols], MULT)
             nc.vector.tensor_tensor(slot[1], window.indirect(pos_sb[1][:, lcols]), gate_sb[1][:, cols], MULT)
-            nc.vector.tensor_tensor(slot[3], window.indirect(cen_sb[:, lcols]), slot[0], ADD)
+            nc.scalar.activation(slot[3], window.indirect(cen_sb[:, lcols]), COPY)
             nc.vector.tensor_tensor(slot[2], window.indirect(pos_sb[2][:, lcols]), gate_sb[2][:, cols], MULT)
-            order = (1, 3, 2)
+            order = (0, 3, 1, 2)
             for k in order:
-                add_turned(slot[k], k == order[0], k == order[2])
+                add_turned(slot[k], k == order[0], k == order[3])
             rows = slice(u * 32, (u + 1) * 32)
             lo = max(c0, PAIRED)
             for b in range(lo // P, c0 // P + blocks):

@@ -16,6 +16,7 @@ FP8X4 = mybir.dt.float8_e4m3fn_x4
 FP4X4 = mybir.dt.float4_e2m1fn_x4
 MULT = mybir.AluOpType.mult
 ADD = mybir.AluOpType.add
+MAX = mybir.AluOpType.max
 COPY = mybir.ActivationFunctionType.Copy
 RELU = mybir.ActivationFunctionType.Relu
 
@@ -26,9 +27,9 @@ BANK = 512
 LIST = 16
 ROW_TILES = H // P
 CHUNKS = ((0, 256), (256, 128), (384, 128))
-FIRST_CUTS = ((0, 512), (512, 768), (768, 1024))
-PAIRED = CHUNKS[1][0]
-QUARTER_CUTS = tuple((lo, lo + 256) for lo in range(0, S, 256))
+WORD_CUTS = ((0, 512), (512, 768), (768, 1024))
+QUARTERS = tuple((lo, lo + 256) for lo in range(0, S, 256))
+PAIRED = 256
 H_SCALE = 0.6 * 0.1
 GATE_SCALE = 0.9 / 0.1
 Z_SCALE = 1.0 / 0.6
@@ -54,57 +55,56 @@ def tile_picked_zgcnii_relu_po_kernel(
 
         xs_raw = keep.tile([P, T], U8, name="xs_raw", align_bytes=64)
         nc.gpsimd.memset(xs_raw[:].bitcast(I32), 0)
-        w2s_raw = keep.tile([P, H], U8, name="w2s_raw", align_bytes=64)
-        nc.gpsimd.memset(w2s_raw[:].bitcast(I32), 0)
         ident = keep.tile([P, P], F32, name="ident")
         make_identity(nc, ident[:])
+        w2s_raw = keep.tile([P, H], U8, name="w2s_raw", align_bytes=64)
+        nc.gpsimd.memset(w2s_raw[:].bitcast(I32), 0)
+        for q in range(4):
+            nc.gpsimd.dma_start(
+                w2s_raw[32 * q : 32 * q + 4, :].bitcast(I32), w2_scales[0, 4 * q : 4 * q + 4, :].bitcast(I32)
+            )
 
         def load_words(g):
             raw = keep.tile([P, T], I32, name=f"xw_raw{g}", align_bytes=64)
             nc.sync.dma_start(raw[:], x_words[g].rearrange("p c r -> p (c r)").bitcast(I32))
             return raw
 
-        h = [keep.tile([P, S], F32, name=f"h{u}") for u in range(ROW_TILES)]
+        h = [keep.tile([P, S], F32, name=f"h{u}", tag=f"h{u % 2}") for u in range(2)]
         w1_raw = {}
 
-        def load_w1(g, u0, tiles, raw):
+        def load_w1(g, u0, raw):
+            tiles = raw.shape[2] // P
             rows = w1[g * P * PACK : (g + 1) * P * PACK, :].rearrange("(p j) c -> p j c", j=PACK)
             nc.sync.dma_start(raw, rows[:, :, u0 * P : (u0 + tiles) * P])
-            w1_raw[g, u0] = raw
+            for k in range(tiles):
+                w1_raw[g, u0 + k] = raw[:, :, k * P : (k + 1) * P]
 
         def own_raw(tag, tiles=1):
             return keep.tile([P, PACK, tiles * P], F32, name=f"raw_{tag}", tag=tag, align_bytes=64)[:]
 
         offs_sb = load_list("offs_sb", offs)
-        w2w_raw = keep.tile([P, 2 * H], U8, name="w2w_raw", align_bytes=64)
-        nc.sync.dma_start(w2w_raw[:].bitcast(I32), w2_words[0].bitcast(I32))
-        gate_cols = keep.tile([P, D, PACK], F32, name="gate_cols")
-        nc.sync.dma_start(gate_cols[:], gate[:, 0, :].rearrange("d (p b) -> p d b", b=PACK))
+        xw_raw = [load_words(0)]
         for q in range(4):
             nc.sync.dma_start(
                 xs_raw[32 * q : 32 * q + 4 * PASSES, :].bitcast(I32),
                 x_scales[:, 4 * q : 4 * q + 4, :].bitcast(I32),
             )
-        xw_raw = [load_words(0)]
-        load_w1(0, 0, 1, own_raw("w1_00"))
-        for q in range(4):
-            nc.sync.dma_start(
-                w2s_raw[32 * q : 32 * q + 4, :].bitcast(I32), w2_scales[0, 4 * q : 4 * q + 4, :].bitcast(I32)
-            )
+        gate_cols = keep.tile([P, D, PACK], F32, name="gate_cols")
+        nc.sync.dma_start(gate_cols[:], gate[:, 0, :].rearrange("d (p b) -> p d b", b=PACK))
+        w2w_raw = keep.tile([P, 2 * H], U8, name="w2w_raw", align_bytes=64)
+        nc.sync.dma_start(w2w_raw[:].bitcast(I32), w2_words[0].bitcast(I32))
+        load_w1(0, 0, own_raw("w1_00"))
         xw_raw.append(load_words(1))
-        load_w1(1, 0, 1, own_raw("before_last_words"))
-        load_w1(0, 1, 1, h[0][:].rearrange("p (j c) -> p j c", j=PACK)[:, :, 0:P])
-        load_w1(1, 1, 1, own_raw("w1_11"))
-        pos_sb = [load_list("pos1_sb", pos1), load_list("pos2_sb", pos2)]
+        pos_sb = [load_list("pos1_sb", pos1), load_list("pos2_sb", pos2), load_list("pos3_sb", pos3)]
         cen_sb = load_list("cen_sb", cen)
-        pos_sb.append(load_list("pos3_sb", pos3))
-        load_w1(0, 2, 2, h[1][:].rearrange("p (j c) -> p j c", j=PACK))
-        load_w1(1, 2, 2, own_raw("before_term1_1", 2))
+        load_w1(1, 0, own_raw("last_words"))
+        load_w1(0, 1, h[0][:].rearrange("p (j c) -> p j c", j=PACK)[:, :, 0:P])
+        load_w1(1, 1, own_raw("w1_11"))
+        load_w1(0, 2, h[1][:].rearrange("p (j c) -> p j c", j=PACK))
+        load_w1(1, 2, own_raw("w1_12"))
+        load_w1(1, 3, own_raw("w1_13"))
         turn_sb = keep.tile([P, PACK], F32, name="turn_sb")
         nc.sync.dma_start(turn_sb[:], turn.rearrange("(p t) o -> p (t o)", t=PACK))
-
-        turn_scaled = keep.tile([P, PACK], F32, name="turn_scaled")
-        nc.scalar.activation(turn_scaled[:], turn_sb[:], COPY, scale=Y_SCALE)
 
         def interleave(planes, packed):
             return (
@@ -112,49 +112,44 @@ def tile_picked_zgcnii_relu_po_kernel(
                 planes.rearrange("p t (c i) -> p c t i", i=4),
             )
 
+        w1_bf = {}
         w1_mx = {}
 
-        def quantise_w1(u0, tiles, tag, passes=(0, 1)):
-            cols = tiles * P
-            count = len(passes)
-            grouped = keep.tile([P, count * cols * PACK], BF16, name=tag + "_bf", tag=tag, align_bytes=64)
-            codes = keep.tile([P, count * cols], U32, name=tag + "_codes", align_bytes=64)
-            scales = keep.tile([P, count * cols], U8, name=tag + "_scales", align_bytes=64)
-            for n, g in enumerate(passes):
-                packed = grouped[:, n * cols * PACK : (n + 1) * cols * PACK].rearrange("p (c j) -> p c j", j=PACK)
-                dst, src = interleave(w1_raw[g, u0], packed)
-                if (g, u0) == (1, 1):
-                    nc.vector.tensor_copy(dst, src)
-                else:
-                    nc.scalar.copy(dst, src)
-                for k in range(tiles):
-                    place = slice(n * cols + k * P, n * cols + (k + 1) * P)
-                    w1_mx[g, u0 + k] = (codes[:, place], scales[:, place])
+        def open_w1(first, count, tag):
+            grouped = keep.tile([P, count * P * PACK], BF16, name=f"w1_bf{first}", tag=tag, align_bytes=64)
+            codes = keep.tile([P, count * P], U32, name=f"w1_codes{first}", align_bytes=64)
+            scales = keep.tile([P, count * P], U8, name=f"w1_scales{first}", align_bytes=64)
+            for k in range(count):
+                u, g = divmod(first + k, PASSES)
+                w1_bf[g, u] = grouped[:, k * P * PACK : (k + 1) * P * PACK].rearrange("p (c j) -> p c j", j=PACK)
+                w1_mx[g, u] = (codes[:, k * P : (k + 1) * P], scales[:, k * P : (k + 1) * P])
+            return grouped, codes, scales
+
+        def round_w1(copy, g, u):
+            copy(*interleave(w1_raw[g, u], w1_bf[g, u]))
+
+        def quantise_w1(grouped, codes, scales):
             nc.vector.quantize_mx(out=codes[:].bitcast(FP8X4), scales=scales[:], in_=grouped[:])
 
-        xs = keep.tile([P, S], U8, name="xs", align_bytes=64)
-        nc.vector.tensor_copy(xs[:], xs_raw[:].indirect(offs_sb[:]))
+        last_lo = WORD_CUTS[-1][0]
         xw0 = keep.tile([P, S], U32, name="xw0", align_bytes=64)
-        nc.vector.tensor_copy(xw0[:], xw_raw[0][:].bitcast(U32).indirect(offs_sb[:]))
-        quantise_w1(0, 1, "w1_bf00", (0,))
-        quantise_w1(0, 1, "w1_bf10", (1,))
-        last_lo = FIRST_CUTS[-1][0]
         xw1 = keep.tile([P, last_lo], U32, name="xw1", align_bytes=64)
-        xw1_last = keep.tile([P, S - last_lo], U32, name="xw1_last", tag="before_last_words", align_bytes=64)
+        xw1_last = keep.tile([P, S - last_lo], U32, name="xw1_last", tag="last_words", align_bytes=64)
+        xs = keep.tile([P, S], U8, name="xs", align_bytes=64)
 
         def words(g, lo, hi):
             if g == 0:
                 return xw0[:, lo:hi]
             return xw1[:, lo:hi] if hi <= last_lo else xw1_last[:, lo - last_lo : hi - last_lo]
 
-        for lo, hi in FIRST_CUTS:
+        def gather_words(g, lo, hi):
             nc.vector.tensor_copy(
-                words(1, lo, hi), xw_raw[1][:].bitcast(U32).indirect(offs_sb[:, lo // LIST : hi // LIST])
+                words(g, lo, hi), xw_raw[g][:].bitcast(U32).indirect(offs_sb[:, lo // LIST : hi // LIST])
             )
 
         gate_sb = [keep.tile([P, V], F32, name=f"gate{d}") for d in range(D)]
 
-        for d in range(D):
+        def spread_gate(d):
             spread = bank(d, [P, PACK, P])
             for b in range(PACK):
                 nc.tensor.transpose(spread[:, b, :], gate_cols[:, d, b : b + 1].to_broadcast([P, P]), ident[:])
@@ -165,36 +160,34 @@ def tile_picked_zgcnii_relu_po_kernel(
                 scale=GATE_SCALE,
             )
 
-        def hidden_rows(u):
-            h_u = h[u]
-            for k, (lo, hi) in enumerate(QUARTER_CUTS if u == 0 else FIRST_CUTS):
-                cols = slice(lo, hi)
-                acc = bank(((3, 4, 5, 7), (0, 1, 2), (3, 4, 5), (0, 1, 2))[u][k], [P, hi - lo])
-                for g in range(PASSES):
-                    codes, scales = w1_mx[g, u]
-                    nc.tensor.matmul_mx(
-                        out=acc[:],
-                        lhsT=codes.bitcast(FP8X4),
-                        lhsT_scale=scales,
-                        rhs=words(g, lo, hi).bitcast(FP8X4),
-                        rhs_scale=xs[4 * g : P, cols],
-                        start=(g == 0),
-                        stop=(g == PASSES - 1),
-                    )
-                nc.scalar.activation(h_u[:, cols], acc[:], RELU, scale=H_SCALE)
+        h_acc = {}
 
-        quantise_w1(1, 1, "before_term0_0")
-        hidden_rows(0)
-        quantise_w1(2, 2, "w1_bf2")
-        hidden_rows(1)
+        def hidden_pass(g, u, cut, k=None):
+            lo, hi = cut
+            if g == 0:
+                h_acc[u, lo] = bank(k, [P, hi - lo])
+            codes, scales = w1_mx[g, u]
+            nc.tensor.matmul_mx(
+                out=h_acc[u, lo][:],
+                lhsT=codes.bitcast(FP8X4),
+                lhsT_scale=scales,
+                rhs=words(g, lo, hi).bitcast(FP8X4),
+                rhs_scale=xs[4 * g : P, lo:hi],
+                start=(g == 0),
+                stop=(g == PASSES - 1),
+            )
 
-        w2w = keep.tile([P, PACK, P, 2], U8, name="w2w", align_bytes=64)
-        nc.vector.tensor_copy(w2w[:], w2w_raw[:].rearrange("p (m t b) -> p t m b", t=PACK, b=2))
-        w2s = keep.tile([P, PACK, P], U8, name="w2s", align_bytes=64)
-        nc.gpsimd.tensor_copy(w2s[:], w2s_raw[:].rearrange("p (m t) -> p t m", t=PACK))
+        def relu(u, cut, on_vector=False):
+            lo, hi = cut
+            if on_vector:
+                nc.vector.tensor_scalar(h[u][:, lo:hi], h_acc[u, lo][:], H_SCALE, 0.0, MULT, MAX)
+            else:
+                nc.scalar.activation(h[u][:, lo:hi], h_acc[u, lo][:], RELU, scale=H_SCALE)
 
-        hidden_rows(2)
-        hidden_rows(3)
+        def hidden_cut(u, cut, k):
+            for g in range(PASSES):
+                hidden_pass(g, u, cut, k)
+            relu(u, cut)
 
         res_flat = keep.tile([P, V * PACK], BF16, name="res_bf", align_bytes=64)
         res_bf = res_flat[:].rearrange("p (c t) -> p c t", t=PACK)
@@ -203,146 +196,137 @@ def tile_picked_zgcnii_relu_po_kernel(
         out_rows = out_0.rearrange("(p t) v -> p t v", t=PACK)
         out_words = out_1[0].rearrange("p c r -> p (c r)").bitcast(I32)
 
-        z_both = keep.tile([P, PACK * V + (V - PAIRED) * 2], F32, name="z_both", tag="w1_bf2", align_bytes=64)
-        z_all = z_both[:, 0 : PACK * V]
-        z_turned = z_all.rearrange("v (b t p) -> v b t p", t=PACK, p=P)
+        terms = {}
+        sums = {}
 
-        z_pairs = z_both[:, PACK * V :]
-        z_pairs_bf = z_pairs.bitcast(BF16).rearrange("v (b w p e) -> v b w p e", w=2, p=P, e=2)
-
-        def mix(u, c0, width, slot, turned):
-            blocks = width // P
+        def gather_term(u, c0, width, d, tag=None, place=None):
             lcols = slice(c0 // LIST, (c0 + width) // LIST)
-            cols = slice(c0, c0 + width)
+            name = f"term{u}_{c0}_{d}"
+            term = place
+            if place is None:
+                term = keep.tile([P, width], F32, name=name, tag=tag or name, align_bytes=64)[:]
+            if d == D:
+                nc.scalar.activation(term, h[u][:].indirect(cen_sb[:, lcols]), COPY)
+            else:
+                nc.vector.tensor_tensor(
+                    term, h[u][:].indirect(pos_sb[d][:, lcols]), gate_sb[d][:, c0 : c0 + width], MULT
+                )
+            terms[u, c0, d] = term
 
-            def add_turned(term, first, final):
-                for b in range(blocks):
+        def gather_gated(u, c0, width, tag=None):
+            for d in range(D):
+                gather_term(u, c0, width, d, tag and f"{tag}{d}")
+
+        def add_terms(u, c0, width, order, first=None, final=False):
+            if first is not None:
+                sums[u, c0] = bank(first, [P, width])
+            for k, d in enumerate(order):
+                for b in range(width // P):
                     nc.tensor.matmul(
-                        turned[:, b * P : (b + 1) * P],
-                        term[:, b * P : (b + 1) * P],
+                        sums[u, c0][:, b * P : (b + 1) * P],
+                        terms[u, c0, d][:, b * P : (b + 1) * P],
                         ident[:],
-                        start=(first and b == 0),
-                        stop=(final and b == blocks - 1),
+                        start=(first is not None and k == 0 and b == 0),
+                        stop=(final and k == len(order) - 1 and b == width // P - 1),
                         is_transpose=True,
                     )
 
-            window = h[u][:]
-            nc.vector.tensor_tensor(slot[0], window.indirect(pos_sb[0][:, lcols]), gate_sb[0][:, cols], MULT)
-            nc.vector.tensor_tensor(slot[1], window.indirect(pos_sb[1][:, lcols]), gate_sb[1][:, cols], MULT)
-            nc.scalar.activation(slot[3], window.indirect(cen_sb[:, lcols]), COPY)
-            nc.vector.tensor_tensor(slot[2], window.indirect(pos_sb[2][:, lcols]), gate_sb[2][:, cols], MULT)
-            order = (0, 3, 1, 2)
-            for k in order:
-                add_turned(slot[k], k == order[0], k == order[3])
-            rows = slice(u * 32, (u + 1) * 32)
-            lo = max(c0, PAIRED)
-            for b in range(lo // P, c0 // P + blocks):
+        def deal_rows(u, c0, width):
+            nc.scalar.copy(
+                z_turned[:, c0 // P : (c0 + width) // P, :, u * 32 : (u + 1) * 32],
+                sums[u, c0][:].rearrange("v (b q t) -> v b t q", t=PACK, q=32),
+            )
+
+
+        def pair_rows(u, c0, width):
+            for b in range(max(c0, PAIRED) // P, (c0 + width) // P):
                 nc.scalar.activation(
-                    z_pairs_bf[:, b - PAIRED // P, :, rows, :],
-                    turned[:, b * P - c0 : (b + 1) * P - c0].rearrange("v (q w e) -> v w q e", w=2, e=2),
+                    z_pairs_bf[:, b - PAIRED // P, :, u * 32 : (u + 1) * 32, :],
+                    sums[u, c0][:, b * P - c0 : (b + 1) * P - c0].rearrange("v (q w e) -> v w q e", w=2, e=2),
                     COPY,
                     scale=Z_SCALE,
                 )
+
+        def turn_pairs(b, k):
+            pairs = bank(k, [P, 2, P])
+            for w in range(2):
+                place = (b * P - PAIRED) * 2 + w * P
+                nc.tensor.transpose(pairs[:, w, :], z_pairs[:, place : place + P], ident[:])
             nc.scalar.copy(
-                z_turned[:, c0 // P : c0 // P + blocks, :, rows],
-                turned.rearrange("v (b q t) -> v b t q", t=PACK, q=32),
+                z_bf[:, b * P * PACK : (b + 1) * P * PACK].bitcast(F32).rearrange("p (v w) -> p v w", w=2),
+                pairs[:].rearrange("p w v -> p v w"),
             )
 
-        def term_slots(name, tag, count, width):
-            terms = keep.tile([P, count * width], F32, name=name, tag=tag, align_bytes=64)
-            return [terms[:, k * width : (k + 1) * width] for k in range(count)]
+        backs = {}
+        z_bf = keep.tile([P, PACK * V], BF16, name="z_bf", align_bytes=64)
+        z_codes = keep.tile([P, V], U32, name="z_codes", align_bytes=64)
+        z_scales = keep.tile([P, V], U8, name="z_scales", align_bytes=64)
 
-        def mix_unit(step, u, c0, width, tag):
-            slot = term_slots(f"terms{step}", tag, D + 1, width)
-            mix(u, c0, width, slot, bank((6, 7, 6, 7, 7, 0)[step], [P, width])[:])
-
-        def quantise_z(n, tag):
-            c0, width = CHUNKS[n]
-            zs = keep.tile([P, PACK, width], F32, name=f"z_scaled{n}")
-            z_flat = keep.tile([P, PACK * width], BF16, name=f"z_bf{n}", tag=tag, align_bytes=64)
-            z_bf = z_flat[:].rearrange("p (c t) -> p c t", t=PACK)
-            z_codes = keep.tile([P, width], U32, name=f"z_codes{n}", align_bytes=64)
-            z_scales = keep.tile([P, width], U8, name=f"z_scales{n}", align_bytes=64)
-            backs = []
-            for b in range(width // P):
-                back = bank(b, [P, PACK, P])
-                for t in range(PACK):
-                    nc.tensor.transpose(back[:, t, :], z_turned[:, c0 // P + b, t, :], ident[:])
-                nc.scalar.activation(
-                    z_bf[:, b * P : (b + 1) * P, :], back[:].rearrange("p t v -> p v t"), COPY, scale=Z_SCALE
-                )
-                backs.append(back)
-            nc.vector.quantize_mx(out=z_codes[:].bitcast(FP8X4), scales=z_scales[:], in_=z_flat[:])
-            return zs, backs, z_codes, z_scales
-
-        def keep_z(zs, backs):
-            for b, back in enumerate(backs):
-                nc.scalar.copy(zs[:, :, b * P : (b + 1) * P], back[:])
-
-        def quantise_pairs(n):
-            c0, width = CHUNKS[n]
-            z_words = keep.tile([P, 2 * width], F32, name=f"z_words{n}", align_bytes=64)
-            z_codes = keep.tile([P, width], U32, name=f"z_codes{n}", align_bytes=64)
-            z_scales = keep.tile([P, width], U8, name=f"z_scales{n}", align_bytes=64)
-            pairs = bank(3 + n, [P, width // P, 2, P])
-            for b in range(width // P):
-                for w in range(2):
-                    place = ((c0 - PAIRED) * 2) + (b * 2 + w) * P
-                    nc.tensor.transpose(pairs[:, b, w, :], z_pairs[:, place : place + P], ident[:])
-            nc.scalar.copy(
-                z_words[:].rearrange("p (b v w) -> p b v w", w=2, v=P), pairs[:].rearrange("p b w v -> p b v w")
-            )
-            nc.vector.quantize_mx(out=z_codes[:].bitcast(FP8X4), scales=z_scales[:], in_=z_words[:].bitcast(BF16))
-            return z_codes, z_scales
-
-        def turn_back(n):
-            c0, width = CHUNKS[n]
-            zs = keep.tile([P, PACK, width], F32, name=f"z_scaled{n}")
-            for b in range(width // P):
-                back = bank((0, 1, 0)[n], [P, PACK, P])
-                for t in range(PACK):
-                    nc.tensor.transpose(back[:, t, :], z_turned[:, c0 // P + b, t, :], ident[:])
-                nc.scalar.copy(zs[:, :, b * P : (b + 1) * P], back[:])
-            return zs
-
-        def second_product(n, z_codes, z_scales):
-            width = CHUNKS[n][1]
-            banks = []
+        def turn_back(b, k):
+            backs[b] = bank(k, [P, PACK, P])
             for t in range(PACK):
-                if n < 2:
-                    y = bank((6, 7, 2, 3)[t], [P, width])
-                else:
-                    if t % 2 == 0:
-                        both = bank(4 + t // 2, [P, 2, width])
-                    y = both[:, t % 2, :]
+                nc.tensor.transpose(backs[b][:, t, :], z_turned[:, b, t, :], ident[:])
+
+        def round_z(b, on_vector=False):
+            dst = z_bf[:, b * P * PACK : (b + 1) * P * PACK].rearrange("p (v t) -> p v t", t=PACK)
+            src = backs[b][:].rearrange("p t v -> p v t")
+            if on_vector:
+                nc.vector.tensor_scalar(dst, src, Z_SCALE, 0.0, MULT, ADD)
+            else:
+                nc.scalar.activation(dst, src, COPY, scale=Z_SCALE)
+
+        def keep_z(b):
+            nc.scalar.copy(z_keep[b // 2][:, b % 2], backs[b][:])
+
+        def quantise_z(n):
+            c0, width = CHUNKS[n]
+            nc.vector.quantize_mx(
+                out=z_codes[:, c0 : c0 + width].bitcast(FP8X4),
+                scales=z_scales[:, c0 : c0 + width],
+                in_=z_bf[:, c0 * PACK : (c0 + width) * PACK],
+            )
+
+        ys = {}
+
+        def second_product(n, banks):
+            c0, width = CHUNKS[n]
+            per = PACK // len(banks)
+            for t in range(PACK):
+                if t % per == 0:
+                    both = bank(banks[t // per], [P, per, width])
+                ys[n, t] = both[:, t % per, :]
                 nc.tensor.matmul_mx(
-                    out=y[:],
+                    out=ys[n, t],
                     lhsT=w2w[:, t, :, :].rearrange("p m b -> p (m b)").bitcast(FP4X4),
                     lhsT_scale=w2s[:, t, :],
-                    rhs=z_codes[:].bitcast(FP8X4),
-                    rhs_scale=z_scales[:],
+                    rhs=z_codes[:, c0 : c0 + width].bitcast(FP8X4),
+                    rhs_scale=z_scales[:, c0 : c0 + width],
                     start=True,
                     stop=True,
                 )
-                banks.append(y[:])
-            return banks
 
-        def combine(n, zs, banks):
+        res = {}
+
+        def combine(n):
             c0, width = CHUNKS[n]
-            res = keep.tile([P, PACK, width], F32, name=f"res{n}")
-            for t, y in enumerate(banks):
+            res[n] = keep.tile([P, PACK, width], F32, name=f"res{n}")
+            for t in range(PACK):
                 nc.vector.scalar_tensor_tensor(
-                    res[:, t, :], y, turn_scaled[:, t : t + 1], zs[:, t, :], MULT, ADD
+                    res[n][:, t, :].rearrange("p (b v) -> p b v", v=P),
+                    ys[n, t].rearrange("p (b v) -> p b v", v=P),
+                    turn_scaled[:, t : t + 1],
+                    z_keep[c0 // (2 * P)][:, c0 // P % 2 : (c0 + width - P) // P % 2 + 1, t, :],
+                    MULT,
+                    ADD,
                 )
-            nc.sync.dma_start(out_rows[:, :, c0 : c0 + width], res[:])
-            return res
+            nc.sync.dma_start(out_rows[:, :, c0 : c0 + width], res[n][:])
 
-        def round_result(copy, n, res, lo, hi):
-            c0 = CHUNKS[n][0]
-            dst, src = interleave(res[:, :, lo:hi], res_bf[:, c0 + lo : c0 + hi, :])
-            copy(dst, src)
+        def round_result(n, copy):
+            c0, width = CHUNKS[n]
+            copy(*interleave(res[n][:], res_bf[:, c0 : c0 + width, :]))
 
-        def result_planes(cols):
+        def result_planes(c0, width):
+            cols = slice(c0, c0 + width)
             nc.vector.quantize_mx(
                 out=out_codes[:, cols].bitcast(FP8X4),
                 scales=out_scales[:, cols],
@@ -350,28 +334,113 @@ def tile_picked_zgcnii_relu_po_kernel(
             )
             nc.sync.dma_start(out_words[:, cols], out_codes[:, cols].bitcast(I32))
 
-        mix_unit(0, 0, 0, V, "before_term0_0")
-        mix_unit(1, 1, 0, V, "before_term1_1")
-        mix_unit(2, 2, *CHUNKS[0], "before_terms2")
-        mix_unit(3, 3, *CHUNKS[0], "terms3")
-        zs0, backs0, z_codes0, z_scales0 = quantise_z(0, "z_bf0")
-        mix_unit(4, 2, PAIRED, V - PAIRED, "terms4")
-        keep_z(zs0, backs0)
-        mix_unit(5, 3, PAIRED, V - PAIRED, "terms5")
-        planes1 = quantise_pairs(1)
-        planes2 = quantise_pairs(2)
-        res0 = combine(0, zs0, second_product(0, z_codes0, z_scales0))
-        zs1 = turn_back(1)
-        zs2 = turn_back(2)
-        round_result(nc.vector.tensor_copy, 0, res0, 0, P)
-        round_result(nc.vector.tensor_copy, 0, res0, P, 2 * P)
-        result_planes(slice(0, 2 * P))
-        res1 = combine(1, zs1, second_product(1, *planes1))
-        res2 = combine(2, zs2, second_product(2, *planes2))
-        round_result(nc.scalar.copy, 1, res1, 0, P)
-        round_result(nc.vector.tensor_copy, 2, res2, 0, P)
-        result_planes(slice(2 * P, 3 * P))
-        result_planes(slice(3 * P, V))
+        gather_words(0, 0, S)
+        nc.vector.tensor_copy(xs[:], xs_raw[:].indirect(offs_sb[:]))
+        for d in range(D):
+            spread_gate(d)
+        w2w = keep.tile([P, PACK, P, 2], U8, name="w2w", align_bytes=64)
+        nc.gpsimd.tensor_copy(w2w[:], w2w_raw[:].rearrange("p (m t b) -> p t m b", t=PACK, b=2))
+        w2s = keep.tile([P, PACK, P], U8, name="w2s", align_bytes=64)
+        nc.gpsimd.tensor_copy(w2s[:], w2s_raw[:].rearrange("p (m t) -> p t m", t=PACK))
+        first = open_w1(0, 1, "w1_bf0")
+        round_w1(nc.scalar.copy, 0, 0)
+        quantise_w1(*first)
+        for k, cut in enumerate(QUARTERS):
+            hidden_pass(0, 0, cut, 4 + k)
+        gather_words(1, *WORD_CUTS[0])
+        gather_words(1, *WORD_CUTS[1])
+        second = open_w1(1, 1, "w1_bf1")
+        round_w1(nc.scalar.copy, 1, 0)
+        quantise_w1(*second)
+        gather_words(1, *WORD_CUTS[2])
+        tile1 = open_w1(2, 2, "first_terms0")
+        round_w1(nc.scalar.copy, 0, 1)
+        round_w1(nc.vector.tensor_copy, 1, 1)
+        quantise_w1(*tile1)
+        for k, cut in enumerate(QUARTERS):
+            hidden_pass(1, 0, cut)
+            relu(0, cut)
+        A, BC = (0, 256), (256, 256)
+        tile2 = open_w1(4, 2, "w1_bf4")
+        tile3 = open_w1(6, 2, "z_all")
+        round_w1(nc.scalar.copy, 0, 2)
+        round_w1(nc.scalar.copy, 0, 3)
+        for k, cut in enumerate(WORD_CUTS):
+            hidden_cut(1, cut, k)
+        gather_gated(0, 0, V, "first_terms")
+        round_w1(nc.scalar.copy, 1, 2)
+        quantise_w1(*tile2)
+        gather_term(1, 0, V, 0, "w1_12")
+        round_w1(nc.scalar.copy, 1, 3)
+        quantise_w1(*tile3)
+        held = keep.tile([P, 3 * V], F32, name="held_terms", tag="w1_13", align_bytes=64)
+        gather_term(1, 0, V, 1, place=held[:, 0:V])
+        gather_term(1, 0, V, 2)
+        gather_term(0, 0, V, D, place=held[:, V : 2 * V])
+        gather_term(1, 0, V, D, place=held[:, 2 * V :])
+        h.extend(keep.tile([P, S], F32, name=f"h{u}", tag=f"h{u % 2}") for u in range(2, ROW_TILES))
+        for k, cut in enumerate(WORD_CUTS):
+            hidden_cut(2, cut, 4 + k)
+        for k, cut in enumerate(WORD_CUTS):
+            hidden_cut(3, cut, k)
+        add_terms(0, 0, V, (0, 1, 2, D), first=3, final=True)
+        add_terms(1, 0, V, (0, 1, D, 2), first=7, final=True)
+        z_all = keep.tile([P, (PACK + 1) * V], F32, name="z_all", align_bytes=64)
+        z_blocks = z_all[:].rearrange("v (b t p) -> v b t p", t=PACK, p=P)
+        z_turned = z_blocks[:, 0:PACK]
+        z_late = keep.tile([P, 2, PACK, P], F32, name="z_late")
+        z_keep = (z_blocks[:, 1 : PACK + 1 : 3], z_late[:])
+        turn_scaled = keep.tile([P, PACK], F32, name="turn_scaled")
+        nc.scalar.activation(turn_scaled[:], turn_sb[:], COPY, scale=Y_SCALE)
+
+        def mix(u, c0, width, k, centre=None):
+            gather_gated(u, c0, width, f"late_terms{u}")
+            gather_term(u, c0, width, D, f"late_centre{u}", centre)
+            add_terms(u, c0, width, (0, 1, 2, D) if centre is None else (D, 0, 1, 2), first=k, final=True)
+
+        deal_rows(0, 0, V)
+        mix(2, *A, 4)
+        deal_rows(1, 0, V)
+        deal_rows(2, *A)
+        mix(3, *A, 5)
+        deal_rows(3, *A)
+        turn_back(0, 0)
+        turn_back(1, 1)
+        round_z(0)
+        mix(2, *BC, 6)
+        last_places = keep.tile([P, 3 * (V - PAIRED)], F32, name="last_places", tag="late_centre3", align_bytes=64)
+        z_pairs = last_places[:, V - PAIRED :]
+        z_pairs_bf = z_pairs.bitcast(BF16).rearrange("v (b w p e) -> v b w p e", w=2, p=P, e=2)
+        mix(3, *BC, 2, last_places[:, 0 : V - PAIRED])
+        pair_rows(0, 0, V)
+        pair_rows(1, 0, V)
+        round_z(1, True)
+        quantise_z(0)
+        pair_rows(2, *BC)
+        pair_rows(3, *BC)
+        keep_z(0)
+        keep_z(1)
+        second_product(0, (3, 7))
+        turn_pairs(2, 4)
+        turn_pairs(3, 5)
+        deal_rows(2, *BC)
+        deal_rows(3, *BC)
+        quantise_z(1)
+        quantise_z(2)
+        combine(0)
+        turn_back(2, 0)
+        turn_back(3, 1)
+        keep_z(2)
+        keep_z(3)
+        round_result(0, nc.vector.tensor_copy)
+        second_product(1, (6, 2))
+        second_product(2, (4, 5))
+        result_planes(*A)
+        combine(1)
+        combine(2)
+        round_result(1, nc.scalar.copy)
+        round_result(2, nc.vector.tensor_copy)
+        result_planes(*BC)
 
         for q in range(4):
             queue = nc.sync if q % 2 == 0 else nc.scalar

@@ -177,6 +177,20 @@ def tile_picked_zgcnii_relu_po_kernel(
                 stop=(g == PASSES - 1),
             )
 
+        def keep_clock(k, passes):
+            unread = bank(k, [P, BANK])
+            codes, scales = w1_mx[0, 0]
+            for n in range(passes):
+                nc.tensor.matmul_mx(
+                    out=unread[:],
+                    lhsT=codes.bitcast(FP8X4),
+                    lhsT_scale=scales,
+                    rhs=xw0[:, 0:BANK].bitcast(FP8X4),
+                    rhs_scale=xs[:, 0:BANK],
+                    start=(n == 0),
+                    stop=(n == passes - 1),
+                )
+
         def relu(u, cut, on_vector=False):
             lo, hi = cut
             if on_vector:
@@ -347,6 +361,7 @@ def tile_picked_zgcnii_relu_po_kernel(
         quantise_w1(*first)
         for k, cut in enumerate(QUARTERS):
             hidden_pass(0, 0, cut, 4 + k)
+        keep_clock(3, 2)
         gather_words(1, *WORD_CUTS[0])
         gather_words(1, *WORD_CUTS[1])
         second = open_w1(1, 1, "w1_bf1")
@@ -420,6 +435,7 @@ def tile_picked_zgcnii_relu_po_kernel(
         pair_rows(3, *BC)
         keep_z(0)
         keep_z(1)
+        keep_clock(3, 1)
         second_product(0, (3, 7))
         turn_pairs(2, 4)
         turn_pairs(3, 5)

@@ -418,6 +418,7 @@ def tile_picked_zgcnii_relu_po_kernel(
         deal_rows(1, 0, V)
         deal_rows(2, *A)
         mix(3, *A, 5)
+        keep_clock(4, 2)
         deal_rows(3, *A)
         turn_back(0, 0)
         turn_back(1, 1)

@@ -361,7 +361,6 @@ def tile_picked_zgcnii_relu_po_kernel(
         quantise_w1(*first)
         for k, cut in enumerate(QUARTERS):
             hidden_pass(0, 0, cut, 4 + k)
-        keep_clock(3, 2)
         gather_words(1, *WORD_CUTS[0])
         gather_words(1, *WORD_CUTS[1])
         second = open_w1(1, 1, "w1_bf1")
@@ -436,7 +435,6 @@ def tile_picked_zgcnii_relu_po_kernel(
         pair_rows(3, *BC)
         keep_z(0)
         keep_z(1)
-        keep_clock(3, 1)
         second_product(0, (3, 7))
         turn_pairs(2, 4)
         turn_pairs(3, 5)

@@ -91,8 +91,6 @@ def tile_picked_zgcnii_relu_po_kernel(
             )
         gate_cols = keep.tile([P, D, PACK], F32, name="gate_cols")
         nc.sync.dma_start(gate_cols[:], gate[:, 0, :].rearrange("d (p b) -> p d b", b=PACK))
-        w2w_raw = keep.tile([P, 2 * H], U8, name="w2w_raw", align_bytes=64)
-        nc.sync.dma_start(w2w_raw[:].bitcast(I32), w2_words[0].bitcast(I32))
         load_w1(0, 0, own_raw("w1_00"))
         xw_raw.append(load_words(1))
         pos_sb = [load_list("pos1_sb", pos1), load_list("pos2_sb", pos2), load_list("pos3_sb", pos3)]
@@ -103,6 +101,8 @@ def tile_picked_zgcnii_relu_po_kernel(
         load_w1(0, 2, h[1][:].rearrange("p (j c) -> p j c", j=PACK))
         load_w1(1, 2, own_raw("w1_12"))
         load_w1(1, 3, own_raw("w1_13"))
+        w2w_raw = keep.tile([P, 2 * H], U8, name="w2w_raw", align_bytes=64)
+        nc.sync.dma_start(w2w_raw[:].bitcast(I32), w2_words[0].bitcast(I32))
         turn_sb = keep.tile([P, PACK], F32, name="turn_sb")
         nc.sync.dma_start(turn_sb[:], turn.rearrange("(p t) o -> p (t o)", t=PACK))
 
@@ -352,8 +352,6 @@ def tile_picked_zgcnii_relu_po_kernel(
         nc.vector.tensor_copy(xs[:], xs_raw[:].indirect(offs_sb[:]))
         for d in range(D):
             spread_gate(d)
-        w2w = keep.tile([P, PACK, P, 2], U8, name="w2w", align_bytes=64)
-        nc.gpsimd.tensor_copy(w2w[:], w2w_raw[:].rearrange("p (m t b) -> p t m b", t=PACK, b=2))
         w2s = keep.tile([P, PACK, P], U8, name="w2s", align_bytes=64)
         nc.gpsimd.tensor_copy(w2s[:], w2s_raw[:].rearrange("p (m t) -> p t m", t=PACK))
         first = open_w1(0, 1, "w1_bf0")
@@ -422,6 +420,11 @@ def tile_picked_zgcnii_relu_po_kernel(
         turn_back(0, 0)
         turn_back(1, 1)
         round_z(0)
+        w2w = keep.tile([P, PACK, P, 2], U8, name="w2w", tag="w1_13", align_bytes=64)
+        nc.scalar.copy(
+            w2w[:].rearrange("p t m b -> p t (m b)").bitcast(U16),
+            w2w_raw[:].bitcast(U16).rearrange("p (m t) -> p t m", t=PACK),
+        )
         mix(2, *BC, 6)
         last_places = keep.tile([P, 3 * (V - PAIRED)], F32, name="last_places", tag="late_centre3", align_bytes=64)
         z_pairs = last_places[:, V - PAIRED :]

@@ -30,6 +30,7 @@ CHUNKS = ((0, 256), (256, 128), (384, 128))
 WORD_CUTS = ((0, 512), (512, 768), (768, 1024))
 QUARTERS = tuple((lo, lo + 256) for lo in range(0, S, 256))
 PAIRED = 256
+WARM_PASSES = 4
 H_SCALE = 0.6 * 0.1
 GATE_SCALE = 0.9 / 0.1
 Z_SCALE = 1.0 / 0.6
@@ -177,18 +178,18 @@ def tile_picked_zgcnii_relu_po_kernel(
                 stop=(g == PASSES - 1),
             )
 
-        def keep_clock(k, passes):
-            unread = bank(k, [P, BANK])
-            codes, scales = w1_mx[0, 0]
-            for n in range(passes):
+        def keep_clock(k, stationary, moving):
+            unread = bank(k, [P, 2, 2 * P])
+            codes, scales = stationary
+            for n in range(WARM_PASSES):
                 nc.tensor.matmul_mx(
-                    out=unread[:],
+                    out=unread[:, n % 2, :],
                     lhsT=codes.bitcast(FP8X4),
                     lhsT_scale=scales,
-                    rhs=xw0[:, 0:BANK].bitcast(FP8X4),
-                    rhs_scale=xs[:, 0:BANK],
-                    start=(n == 0),
-                    stop=(n == passes - 1),
+                    rhs=moving[1][:].bitcast(FP8X4),
+                    rhs_scale=moving[2][:],
+                    start=True,
+                    stop=True,
                 )
 
         def relu(u, cut, on_vector=False):
@@ -415,7 +416,7 @@ def tile_picked_zgcnii_relu_po_kernel(
         deal_rows(1, 0, V)
         deal_rows(2, *A)
         mix(3, *A, 5)
-        keep_clock(4, 2)
+        keep_clock(4, w1_mx[0, 0], tile2)
         deal_rows(3, *A)
         turn_back(0, 0)
         turn_back(1, 1)

@@ -30,7 +30,7 @@ CHUNKS = ((0, 256), (256, 128), (384, 128))
 WORD_CUTS = ((0, 512), (512, 768), (768, 1024))
 QUARTERS = tuple((lo, lo + 256) for lo in range(0, S, 256))
 PAIRED = 256
-WARM_PASSES = 4
+WARM_PASSES = 2
 H_SCALE = 0.6 * 0.1
 GATE_SCALE = 0.9 / 0.1
 Z_SCALE = 1.0 / 0.6
@@ -116,10 +116,14 @@ def tile_picked_zgcnii_relu_po_kernel(
         w1_bf = {}
         w1_mx = {}
 
-        def open_w1(first, count, tag):
-            grouped = keep.tile([P, count * P * PACK], BF16, name=f"w1_bf{first}", tag=tag, align_bytes=64)
+        def open_planes(first, count):
             codes = keep.tile([P, count * P], U32, name=f"w1_codes{first}", align_bytes=64)
             scales = keep.tile([P, count * P], U8, name=f"w1_scales{first}", align_bytes=64)
+            return codes[:], scales[:]
+
+        def open_w1(first, count, tag, planes=None):
+            grouped = keep.tile([P, count * P * PACK], BF16, name=f"w1_bf{first}", tag=tag, align_bytes=64)
+            codes, scales = planes or open_planes(first, count)
             for k in range(count):
                 u, g = divmod(first + k, PASSES)
                 w1_bf[g, u] = grouped[:, k * P * PACK : (k + 1) * P * PACK].rearrange("p (c j) -> p c j", j=PACK)
@@ -130,7 +134,7 @@ def tile_picked_zgcnii_relu_po_kernel(
             copy(*interleave(w1_raw[g, u], w1_bf[g, u]))
 
         def quantise_w1(grouped, codes, scales):
-            nc.vector.quantize_mx(out=codes[:].bitcast(FP8X4), scales=scales[:], in_=grouped[:])
+            nc.vector.quantize_mx(out=codes.bitcast(FP8X4), scales=scales, in_=grouped[:])
 
         last_lo = WORD_CUTS[-1][0]
         xw0 = keep.tile([P, S], U32, name="xw0", align_bytes=64)
@@ -179,17 +183,17 @@ def tile_picked_zgcnii_relu_po_kernel(
             )
 
         def keep_clock(k, stationary, moving):
-            unread = bank(k, [P, 2, 2 * P])
+            unread = bank(k, [P, BANK])
             codes, scales = stationary
             for n in range(WARM_PASSES):
                 nc.tensor.matmul_mx(
-                    out=unread[:, n % 2, :],
+                    out=unread[:],
                     lhsT=codes.bitcast(FP8X4),
                     lhsT_scale=scales,
-                    rhs=moving[1][:].bitcast(FP8X4),
-                    rhs_scale=moving[2][:],
-                    start=True,
-                    stop=True,
+                    rhs=moving[0].bitcast(FP8X4),
+                    rhs_scale=moving[1],
+                    start=(n == 0),
+                    stop=(n == WARM_PASSES - 1),
                 )
 
         def relu(u, cut, on_vector=False):
@@ -374,8 +378,9 @@ def tile_picked_zgcnii_relu_po_kernel(
             hidden_pass(1, 0, cut)
             relu(0, cut)
         A, BC = (0, 256), (256, 256)
-        tile2 = open_w1(4, 2, "w1_bf4")
-        tile3 = open_w1(6, 2, "z_all")
+        late = open_planes(4, 4)
+        tile2 = open_w1(4, 2, "w1_bf4", [plane[:, 0 : 2 * P] for plane in late])
+        tile3 = open_w1(6, 2, "z_all", [plane[:, 2 * P :] for plane in late])
         round_w1(nc.scalar.copy, 0, 2)
         round_w1(nc.scalar.copy, 0, 3)
         for k, cut in enumerate(WORD_CUTS):
@@ -416,7 +421,7 @@ def tile_picked_zgcnii_relu_po_kernel(
         deal_rows(1, 0, V)
         deal_rows(2, *A)
         mix(3, *A, 5)
-        keep_clock(4, w1_mx[0, 0], tile2)
+        keep_clock(4, w1_mx[0, 0], late)
         deal_rows(3, *A)
         turn_back(0, 0)
         turn_back(1, 1)

@@ -294,8 +294,8 @@ def tile_picked_zgcnii_relu_po_kernel(
             else:
                 nc.scalar.activation(dst, src, COPY, scale=Z_SCALE)
 
-        def keep_z(b):
-            nc.scalar.copy(z_keep[b // 2][:, b % 2], backs[b][:])
+        def keep_z(b, copy=nc.scalar.copy):
+            copy(z_keep[b // 2][:, b % 2], backs[b][:])
 
         def quantise_z(n):
             c0, width = CHUNKS[n]
@@ -396,7 +396,7 @@ def tile_picked_zgcnii_relu_po_kernel(
         gather_term(1, 0, V, 2)
         gather_term(0, 0, V, D, place=held[:, V : 2 * V])
         gather_term(1, 0, V, D, place=held[:, 2 * V :])
-        h.extend(keep.tile([P, S], F32, name=f"h{u}", tag=f"h{u % 2}") for u in range(2, ROW_TILES))
+        h.extend(keep.tile([P, S], F32, name=f"h{u}", tag=("h0", "h3")[u % 2]) for u in range(2, ROW_TILES))
         for k, cut in enumerate(WORD_CUTS):
             hidden_cut(2, cut, 4 + k)
         for k, cut in enumerate(WORD_CUTS):
@@ -426,6 +426,7 @@ def tile_picked_zgcnii_relu_po_kernel(
         turn_back(0, 0)
         turn_back(1, 1)
         round_z(0)
+        round_z(1)
         w2w = keep.tile([P, PACK, P, 2], U8, name="w2w", tag="w1_13", align_bytes=64)
         nc.scalar.copy(
             w2w[:].rearrange("p t m b -> p t (m b)").bitcast(U16),
@@ -438,11 +439,10 @@ def tile_picked_zgcnii_relu_po_kernel(
         mix(3, *BC, 2, last_places[:, 0 : V - PAIRED])
         pair_rows(0, 0, V)
         pair_rows(1, 0, V)
-        round_z(1, True)
         quantise_z(0)
+        keep_z(0, nc.vector.tensor_copy)
         pair_rows(2, *BC)
         pair_rows(3, *BC)
-        keep_z(0)
         keep_z(1)
         second_product(0, (3, 7))
         turn_pairs(2, 4)

@@ -208,8 +208,6 @@ def tile_picked_zgcnii_relu_po_kernel(
                 hidden_pass(g, u, cut, k)
             relu(u, cut)
 
-        res_flat = keep.tile([P, V * PACK], BF16, name="res_bf", align_bytes=64)
-        res_bf = res_flat[:].rearrange("p (c t) -> p c t", t=PACK)
         out_codes = keep.tile([P, V], U32, name="out_codes", align_bytes=64)
         out_scales = keep.tile([P, V], U8, name="out_scales", align_bytes=64)
         out_rows = out_0.rearrange("(p t) v -> p t v", t=PACK)
@@ -433,37 +431,39 @@ def tile_picked_zgcnii_relu_po_kernel(
             w2w_raw[:].bitcast(U16).rearrange("p (m t) -> p t m", t=PACK),
         )
         mix(2, *BC, 6)
-        last_places = keep.tile([P, 3 * (V - PAIRED)], F32, name="last_places", tag="late_centre3", align_bytes=64)
-        z_pairs = last_places[:, V - PAIRED :]
+        last_centre = keep.tile([P, V - PAIRED], F32, name="last_centre", tag="late_centre3", align_bytes=64)
+        z_pairs = z_all[:, 0 : 2 * (V - PAIRED)]
         z_pairs_bf = z_pairs.bitcast(BF16).rearrange("v (b w p e) -> v b w p e", w=2, p=P, e=2)
-        mix(3, *BC, 2, last_places[:, 0 : V - PAIRED])
+        mix(3, *BC, 2, last_centre[:])
         pair_rows(0, 0, V)
         pair_rows(1, 0, V)
         quantise_z(0)
         keep_z(0, nc.vector.tensor_copy)
         pair_rows(2, *BC)
+        deal_rows(2, *BC)
+        keep_z(1, nc.vector.tensor_copy)
         pair_rows(3, *BC)
-        keep_z(1)
+        deal_rows(3, *BC)
         second_product(0, (3, 7))
         turn_pairs(2, 4)
         turn_pairs(3, 5)
-        deal_rows(2, *BC)
-        deal_rows(3, *BC)
-        quantise_z(1)
-        quantise_z(2)
         combine(0)
+        quantise_z(1)
         turn_back(2, 0)
         turn_back(3, 1)
         keep_z(2)
         keep_z(3)
-        round_result(0, nc.vector.tensor_copy)
         second_product(1, (6, 2))
+        quantise_z(2)
         second_product(2, (4, 5))
-        result_planes(*A)
+        res_flat = keep.tile([P, V * PACK], BF16, name="res_bf", tag="z_all", align_bytes=64)
+        res_bf = res_flat[:].rearrange("p (c t) -> p c t", t=PACK)
+        round_result(0, nc.scalar.copy)
         combine(1)
         combine(2)
-        round_result(1, nc.scalar.copy)
+        round_result(1, nc.vector.tensor_copy)
         round_result(2, nc.vector.tensor_copy)
+        result_planes(*A)
         result_planes(*BC)
 
         for q in range(4):

from contextlib import ExitStack

import concourse.mybir as mybir
from concourse.masks import make_identity

K, T, S, D, V, H = 1024, 2048, 1024, 3, 512, 512
FLOPS = 2 * K * H * S + 2 * H * H * V

F32 = mybir.dt.float32
BF16 = mybir.dt.bfloat16
I32 = mybir.dt.int32
U32 = mybir.dt.uint32
U16 = mybir.dt.uint16
U8 = mybir.dt.uint8
FP8X4 = mybir.dt.float8_e4m3fn_x4
FP4X4 = mybir.dt.float4_e2m1fn_x4
MULT = mybir.AluOpType.mult
ADD = mybir.AluOpType.add
MAX = mybir.AluOpType.max
COPY = mybir.ActivationFunctionType.Copy
RELU = mybir.ActivationFunctionType.Relu

P = 128
PACK = 4
PASSES = K // (P * PACK)
BANK = 512
LIST = 16
ROW_TILES = H // P
CHUNKS = ((0, 256), (256, 128), (384, 128))
WORD_CUTS = ((0, 512), (512, 768), (768, 1024))
QUARTERS = tuple((lo, lo + 256) for lo in range(0, S, 256))
PAIRED = 256
WARM_PASSES = 2
H_SCALE = 0.6 * 0.1
GATE_SCALE = 0.9 / 0.1
Z_SCALE = 1.0 / 0.6
Y_SCALE = 0.4


def tile_picked_zgcnii_relu_po_kernel(
    tc, x_words, x_scales, w1, w2_words, w2_scales, gate, turn, offs, cen, pos1, pos2, pos3, out_0, out_1, out_2
):
    nc = tc.nc
    with ExitStack() as ctx:
        lists = ctx.enter_context(tc.tile_pool(name="lists", bufs=1))
        keep = ctx.enter_context(tc.tile_pool(name="keep", bufs=1))
        psum = ctx.enter_context(tc.psum_pool(name="psum", bufs=1))

        def bank(k, shape):
            return psum.tile(shape, F32, name=f"bank{k}")

        def load_list(name, src):
            held = lists.tile([P, src.shape[1]], U16, name=name)
            nc.sync.dma_start(held[:], src)
            return held

        xs_raw = keep.tile([P, T], U8, name="xs_raw", align_bytes=64)
        nc.gpsimd.memset(xs_raw[:].bitcast(I32), 0)
        ident = keep.tile([P, P], F32, name="ident")
        make_identity(nc, ident[:])
        w2s_raw = keep.tile([P, H], U8, name="w2s_raw", align_bytes=64)
        nc.gpsimd.memset(w2s_raw[:].bitcast(I32), 0)
        for q in range(4):
            nc.gpsimd.dma_start(
                w2s_raw[32 * q : 32 * q + 4, :].bitcast(I32), w2_scales[0, 4 * q : 4 * q + 4, :].bitcast(I32)
            )

        def load_words(g):
            raw = keep.tile([P, T], I32, name=f"xw_raw{g}", align_bytes=64)
            nc.sync.dma_start(raw[:], x_words[g].rearrange("p c r -> p (c r)").bitcast(I32))
            return raw

        h = [keep.tile([P, S], F32, name=f"h{u}", tag=f"h{u % 2}") for u in range(2)]
        w1_raw = {}

        def load_w1(g, u0, raw):
            tiles = raw.shape[2] // P
            rows = w1[g * P * PACK : (g + 1) * P * PACK, :].rearrange("(p j) c -> p j c", j=PACK)
            nc.sync.dma_start(raw, rows[:, :, u0 * P : (u0 + tiles) * P])
            for k in range(tiles):
                w1_raw[g, u0 + k] = raw[:, :, k * P : (k + 1) * P]

        def own_raw(tag, tiles=1):
            return keep.tile([P, PACK, tiles * P], F32, name=f"raw_{tag}", tag=tag, align_bytes=64)[:]

        offs_sb = load_list("offs_sb", offs)
        xw_raw = [load_words(0)]
        for q in range(4):
            nc.sync.dma_start(
                xs_raw[32 * q : 32 * q + 4 * PASSES, :].bitcast(I32),
                x_scales[:, 4 * q : 4 * q + 4, :].bitcast(I32),
            )
        gate_cols = keep.tile([P, D, PACK], F32, name="gate_cols")
        nc.sync.dma_start(gate_cols[:], gate[:, 0, :].rearrange("d (p b) -> p d b", b=PACK))
        load_w1(0, 0, own_raw("w1_00"))
        xw_raw.append(load_words(1))
        pos_sb = [load_list("pos1_sb", pos1), load_list("pos2_sb", pos2), load_list("pos3_sb", pos3)]
        cen_sb = load_list("cen_sb", cen)
        load_w1(1, 0, own_raw("last_words"))
        load_w1(0, 1, h[0][:].rearrange("p (j c) -> p j c", j=PACK)[:, :, 0:P])
        load_w1(1, 1, own_raw("w1_11"))
        load_w1(0, 2, h[1][:].rearrange("p (j c) -> p j c", j=PACK))
        load_w1(1, 2, own_raw("w1_12"))
        load_w1(1, 3, own_raw("w1_13"))
        w2w_raw = keep.tile([P, 2 * H], U8, name="w2w_raw", align_bytes=64)
        nc.sync.dma_start(w2w_raw[:].bitcast(I32), w2_words[0].bitcast(I32))
        turn_sb = keep.tile([P, PACK], F32, name="turn_sb")
        nc.sync.dma_start(turn_sb[:], turn.rearrange("(p t) o -> p (t o)", t=PACK))

        def interleave(planes, packed):
            return (
                packed.rearrange("p (c i) t -> p c t i", i=4),
                planes.rearrange("p t (c i) -> p c t i", i=4),
            )

        w1_bf = {}
        w1_mx = {}

        def open_planes(first, count):
            codes = keep.tile([P, count * P], U32, name=f"w1_codes{first}", align_bytes=64)
            scales = keep.tile([P, count * P], U8, name=f"w1_scales{first}", align_bytes=64)
            return codes[:], scales[:]

        def open_w1(first, count, tag, planes=None):
            grouped = keep.tile([P, count * P * PACK], BF16, name=f"w1_bf{first}", tag=tag, align_bytes=64)
            codes, scales = planes or open_planes(first, count)
            for k in range(count):
                u, g = divmod(first + k, PASSES)
                w1_bf[g, u] = grouped[:, k * P * PACK : (k + 1) * P * PACK].rearrange("p (c j) -> p c j", j=PACK)
                w1_mx[g, u] = (codes[:, k * P : (k + 1) * P], scales[:, k * P : (k + 1) * P])
            return grouped, codes, scales

        def round_w1(copy, g, u):
            copy(*interleave(w1_raw[g, u], w1_bf[g, u]))

        def quantise_w1(grouped, codes, scales):
            nc.vector.quantize_mx(out=codes.bitcast(FP8X4), scales=scales, in_=grouped[:])

        last_lo = WORD_CUTS[-1][0]
        xw0 = keep.tile([P, S], U32, name="xw0", align_bytes=64)
        xw1 = keep.tile([P, last_lo], U32, name="xw1", align_bytes=64)
        xw1_last = keep.tile([P, S - last_lo], U32, name="xw1_last", tag="last_words", align_bytes=64)
        xs = keep.tile([P, S], U8, name="xs", align_bytes=64)

        def words(g, lo, hi):
            if g == 0:
                return xw0[:, lo:hi]
            return xw1[:, lo:hi] if hi <= last_lo else xw1_last[:, lo - last_lo : hi - last_lo]

        def gather_words(g, lo, hi):
            nc.vector.tensor_copy(
                words(g, lo, hi), xw_raw[g][:].bitcast(U32).indirect(offs_sb[:, lo // LIST : hi // LIST])
            )

        gate_sb = [keep.tile([P, V], F32, name=f"gate{d}") for d in range(D)]

        def spread_gate(d):
            spread = bank(d, [P, PACK, P])
            for b in range(PACK):
                nc.tensor.transpose(spread[:, b, :], gate_cols[:, d, b : b + 1].to_broadcast([P, P]), ident[:])
            nc.scalar.activation(
                gate_sb[d][:].rearrange("p (n b) -> p n b", b=PACK),
                spread[:].rearrange("p b n -> p n b"),
                COPY,
                scale=GATE_SCALE,
            )

        h_acc = {}

        def hidden_pass(g, u, cut, k=None):
            lo, hi = cut
            if g == 0:
                h_acc[u, lo] = bank(k, [P, hi - lo])
            codes, scales = w1_mx[g, u]
            nc.tensor.matmul_mx(
                out=h_acc[u, lo][:],
                lhsT=codes.bitcast(FP8X4),
                lhsT_scale=scales,
                rhs=words(g, lo, hi).bitcast(FP8X4),
                rhs_scale=xs[4 * g : P, lo:hi],
                start=(g == 0),
                stop=(g == PASSES - 1),
            )

        def keep_clock(k, stationary, moving):
            unread = bank(k, [P, BANK])
            codes, scales = stationary
            for n in range(WARM_PASSES):
                nc.tensor.matmul_mx(
                    out=unread[:],
                    lhsT=codes.bitcast(FP8X4),
                    lhsT_scale=scales,
                    rhs=moving[0].bitcast(FP8X4),
                    rhs_scale=moving[1],
                    start=(n == 0),
                    stop=(n == WARM_PASSES - 1),
                )

        def relu(u, cut, on_vector=False):
            lo, hi = cut
            if on_vector:
                nc.vector.tensor_scalar(h[u][:, lo:hi], h_acc[u, lo][:], H_SCALE, 0.0, MULT, MAX)
            else:
                nc.scalar.activation(h[u][:, lo:hi], h_acc[u, lo][:], RELU, scale=H_SCALE)

        def hidden_cut(u, cut, k):
            for g in range(PASSES):
                hidden_pass(g, u, cut, k)
            relu(u, cut)

        out_codes = keep.tile([P, V], U32, name="out_codes", align_bytes=64)
        out_scales = keep.tile([P, V], U8, name="out_scales", align_bytes=64)
        out_rows = out_0.rearrange("(p t) v -> p t v", t=PACK)
        out_words = out_1[0].rearrange("p c r -> p (c r)").bitcast(I32)

        terms = {}
        sums = {}

        def gather_term(u, c0, width, d, tag=None, place=None):
            lcols = slice(c0 // LIST, (c0 + width) // LIST)
            name = f"term{u}_{c0}_{d}"
            term = place
            if place is None:
                term = keep.tile([P, width], F32, name=name, tag=tag or name, align_bytes=64)[:]
            if d == D:
                nc.scalar.activation(term, h[u][:].indirect(cen_sb[:, lcols]), COPY)
            else:
                nc.vector.tensor_tensor(
                    term, h[u][:].indirect(pos_sb[d][:, lcols]), gate_sb[d][:, c0 : c0 + width], MULT
                )
            terms[u, c0, d] = term

        def gather_gated(u, c0, width, tag=None):
            for d in range(D):
                gather_term(u, c0, width, d, tag and f"{tag}{d}")

        def add_terms(u, c0, width, order, first=None, final=False):
            if first is not None:
                sums[u, c0] = bank(first, [P, width])
            for k, d in enumerate(order):
                for b in range(width // P):
                    nc.tensor.matmul(
                        sums[u, c0][:, b * P : (b + 1) * P],
                        terms[u, c0, d][:, b * P : (b + 1) * P],
                        ident[:],
                        start=(first is not None and k == 0 and b == 0),
                        stop=(final and k == len(order) - 1 and b == width // P - 1),
                        is_transpose=True,
                    )

        def deal_rows(u, c0, width):
            nc.scalar.copy(
                z_turned[:, c0 // P : (c0 + width) // P, :, u * 32 : (u + 1) * 32],
                sums[u, c0][:].rearrange("v (b q t) -> v b t q", t=PACK, q=32),
            )


        def pair_rows(u, c0, width):
            for b in range(max(c0, PAIRED) // P, (c0 + width) // P):
                nc.scalar.activation(
                    z_pairs_bf[:, b - PAIRED // P, :, u * 32 : (u + 1) * 32, :],
                    sums[u, c0][:, b * P - c0 : (b + 1) * P - c0].rearrange("v (q w e) -> v w q e", w=2, e=2),
                    COPY,
                    scale=Z_SCALE,
                )

        def turn_pairs(b, k):
            pairs = bank(k, [P, 2, P])
            for w in range(2):
                place = (b * P - PAIRED) * 2 + w * P
                nc.tensor.transpose(pairs[:, w, :], z_pairs[:, place : place + P], ident[:])
            nc.scalar.copy(
                z_bf[:, b * P * PACK : (b + 1) * P * PACK].bitcast(F32).rearrange("p (v w) -> p v w", w=2),
                pairs[:].rearrange("p w v -> p v w"),
            )

        backs = {}
        z_bf = keep.tile([P, PACK * V], BF16, name="z_bf", align_bytes=64)
        z_codes = keep.tile([P, V], U32, name="z_codes", align_bytes=64)
        z_scales = keep.tile([P, V], U8, name="z_scales", align_bytes=64)

        def turn_back(b, k):
            backs[b] = bank(k, [P, PACK, P])
            for t in range(PACK):
                nc.tensor.transpose(backs[b][:, t, :], z_turned[:, b, t, :], ident[:])

        def round_z(b, on_vector=False):
            dst = z_bf[:, b * P * PACK : (b + 1) * P * PACK].rearrange("p (v t) -> p v t", t=PACK)
            src = backs[b][:].rearrange("p t v -> p v t")
            if on_vector:
                nc.vector.tensor_scalar(dst, src, Z_SCALE, 0.0, MULT, ADD)
            else:
                nc.scalar.activation(dst, src, COPY, scale=Z_SCALE)

        def keep_z(b, copy=nc.scalar.copy):
            copy(z_keep[b // 2][:, b % 2], backs[b][:])

        def quantise_z(n):
            c0, width = CHUNKS[n]
            nc.vector.quantize_mx(
                out=z_codes[:, c0 : c0 + width].bitcast(FP8X4),
                scales=z_scales[:, c0 : c0 + width],
                in_=z_bf[:, c0 * PACK : (c0 + width) * PACK],
            )

        ys = {}

        def second_product(n, banks):
            c0, width = CHUNKS[n]
            per = PACK // len(banks)
            for t in range(PACK):
                if t % per == 0:
                    both = bank(banks[t // per], [P, per, width])
                ys[n, t] = both[:, t % per, :]
                nc.tensor.matmul_mx(
                    out=ys[n, t],
                    lhsT=w2w[:, t, :, :].rearrange("p m b -> p (m b)").bitcast(FP4X4),
                    lhsT_scale=w2s[:, t, :],
                    rhs=z_codes[:, c0 : c0 + width].bitcast(FP8X4),
                    rhs_scale=z_scales[:, c0 : c0 + width],
                    start=True,
                    stop=True,
                )

        res = {}

        def combine(n):
            c0, width = CHUNKS[n]
            res[n] = keep.tile([P, PACK, width], F32, name=f"res{n}")
            for t in range(PACK):
                nc.vector.scalar_tensor_tensor(
                    res[n][:, t, :].rearrange("p (b v) -> p b v", v=P),
                    ys[n, t].rearrange("p (b v) -> p b v", v=P),
                    turn_scaled[:, t : t + 1],
                    z_keep[c0 // (2 * P)][:, c0 // P % 2 : (c0 + width - P) // P % 2 + 1, t, :],
                    MULT,
                    ADD,
                )
            nc.sync.dma_start(out_rows[:, :, c0 : c0 + width], res[n][:])

        def round_result(n, copy):
            c0, width = CHUNKS[n]
            copy(*interleave(res[n][:], res_bf[:, c0 : c0 + width, :]))

        def result_planes(c0, width):
            cols = slice(c0, c0 + width)
            nc.vector.quantize_mx(
                out=out_codes[:, cols].bitcast(FP8X4),
                scales=out_scales[:, cols],
                in_=res_bf[:, cols, :].rearrange("p c t -> p (c t)"),
            )
            nc.sync.dma_start(out_words[:, cols], out_codes[:, cols].bitcast(I32))

        gather_words(0, 0, S)
        nc.vector.tensor_copy(xs[:], xs_raw[:].indirect(offs_sb[:]))
        for d in range(D):
            spread_gate(d)
        w2s = keep.tile([P, PACK, P], U8, name="w2s", align_bytes=64)
        nc.gpsimd.tensor_copy(w2s[:], w2s_raw[:].rearrange("p (m t) -> p t m", t=PACK))
        first = open_w1(0, 1, "w1_bf0")
        round_w1(nc.scalar.copy, 0, 0)
        quantise_w1(*first)
        for k, cut in enumerate(QUARTERS):
            hidden_pass(0, 0, cut, 4 + k)
        gather_words(1, *WORD_CUTS[0])
        gather_words(1, *WORD_CUTS[1])
        second = open_w1(1, 1, "w1_bf1")
        round_w1(nc.scalar.copy, 1, 0)
        quantise_w1(*second)
        gather_words(1, *WORD_CUTS[2])
        tile1 = open_w1(2, 2, "first_terms0")
        round_w1(nc.scalar.copy, 0, 1)
        round_w1(nc.vector.tensor_copy, 1, 1)
        quantise_w1(*tile1)
        for k, cut in enumerate(QUARTERS):
            hidden_pass(1, 0, cut)
            relu(0, cut)
        A, BC = (0, 256), (256, 256)
        late = open_planes(4, 4)
        tile2 = open_w1(4, 2, "w1_bf4", [plane[:, 0 : 2 * P] for plane in late])
        tile3 = open_w1(6, 2, "z_all", [plane[:, 2 * P :] for plane in late])
        round_w1(nc.scalar.copy, 0, 2)
        round_w1(nc.scalar.copy, 0, 3)
        for k, cut in enumerate(WORD_CUTS):
            hidden_cut(1, cut, k)
        gather_gated(0, 0, V, "first_terms")
        round_w1(nc.scalar.copy, 1, 2)
        quantise_w1(*tile2)
        gather_term(1, 0, V, 0, "w1_12")
        round_w1(nc.scalar.copy, 1, 3)
        quantise_w1(*tile3)
        held = keep.tile([P, 3 * V], F32, name="held_terms", tag="w1_13", align_bytes=64)
        gather_term(1, 0, V, 1, place=held[:, 0:V])
        gather_term(1, 0, V, 2)
        gather_term(0, 0, V, D, place=held[:, V : 2 * V])
        gather_term(1, 0, V, D, place=held[:, 2 * V :])
        h.extend(keep.tile([P, S], F32, name=f"h{u}", tag=("h0", "h3")[u % 2]) for u in range(2, ROW_TILES))
        for k, cut in enumerate(WORD_CUTS):
            hidden_cut(2, cut, 4 + k)
        for k, cut in enumerate(WORD_CUTS):
            hidden_cut(3, cut, k)
        add_terms(0, 0, V, (0, 1, 2, D), first=3, final=True)
        add_terms(1, 0, V, (0, 1, D, 2), first=7, final=True)
        z_all = keep.tile([P, (PACK + 1) * V], F32, name="z_all", align_bytes=64)
        z_blocks = z_all[:].rearrange("v (b t p) -> v b t p", t=PACK, p=P)
        z_turned = z_blocks[:, 0:PACK]
        z_late = keep.tile([P, 2, PACK, P], F32, name="z_late")
        z_keep = (z_blocks[:, 1 : PACK + 1 : 3], z_late[:])
        turn_scaled = keep.tile([P, PACK], F32, name="turn_scaled")
        nc.scalar.activation(turn_scaled[:], turn_sb[:], COPY, scale=Y_SCALE)

        def mix(u, c0, width, k, centre=None):
            gather_gated(u, c0, width, f"late_terms{u}")
            gather_term(u, c0, width, D, f"late_centre{u}", centre)
            add_terms(u, c0, width, (0, 1, 2, D) if centre is None else (D, 0, 1, 2), first=k, final=True)

        deal_rows(0, 0, V)
        mix(2, *A, 4)
        deal_rows(1, 0, V)
        deal_rows(2, *A)
        mix(3, *A, 5)
        keep_clock(4, w1_mx[0, 0], late)
        deal_rows(3, *A)
        turn_back(0, 0)
        turn_back(1, 1)
        round_z(0)
        round_z(1)
        w2w = keep.tile([P, PACK, P, 2], U8, name="w2w", tag="w1_13", align_bytes=64)
        nc.scalar.copy(
            w2w[:].rearrange("p t m b -> p t (m b)").bitcast(U16),
            w2w_raw[:].bitcast(U16).rearrange("p (m t) -> p t m", t=PACK),
        )
        mix(2, *BC, 6)
        last_centre = keep.tile([P, V - PAIRED], F32, name="last_centre", tag="late_centre3", align_bytes=64)
        z_pairs = z_all[:, 0 : 2 * (V - PAIRED)]
        z_pairs_bf = z_pairs.bitcast(BF16).rearrange("v (b w p e) -> v b w p e", w=2, p=P, e=2)
        mix(3, *BC, 2, last_centre[:])
        pair_rows(0, 0, V)
        pair_rows(1, 0, V)
        quantise_z(0)
        keep_z(0, nc.vector.tensor_copy)
        pair_rows(2, *BC)
        deal_rows(2, *BC)
        keep_z(1, nc.vector.tensor_copy)
        pair_rows(3, *BC)
        deal_rows(3, *BC)
        second_product(0, (3, 7))
        turn_pairs(2, 4)
        turn_pairs(3, 5)
        combine(0)
        quantise_z(1)
        turn_back(2, 0)
        turn_back(3, 1)
        keep_z(2)
        keep_z(3)
        second_product(1, (6, 2))
        quantise_z(2)
        second_product(2, (4, 5))
        res_flat = keep.tile([P, V * PACK], BF16, name="res_bf", tag="z_all", align_bytes=64)
        res_bf = res_flat[:].rearrange("p (c t) -> p c t", t=PACK)
        round_result(0, nc.scalar.copy)
        combine(1)
        combine(2)
        round_result(1, nc.vector.tensor_copy)
        round_result(2, nc.vector.tensor_copy)
        result_planes(*A)
        result_planes(*BC)

        for q in range(4):
            queue = nc.sync if q % 2 == 0 else nc.scalar
            queue.dma_start(
                out_2[0, 4 * q : 4 * q + 4, :].bitcast(I32), out_scales[32 * q : 32 * q + 4, :].bitcast(I32)
            )
